import numpy as np
import ml_dtypes


def mxq(x, axis, fmt="e4m3"):
    dtype, down = {"e4m3": (ml_dtypes.float8_e4m3fn, 7), "e5m2": (ml_dtypes.float8_e5m2, 14)}[fmt]
    v = np.moveaxis(np.asarray(x, np.float32).astype(ml_dtypes.bfloat16).astype(np.float64), axis, -1)
    blocks = v.reshape(v.shape[:-1] + (-1, 32))
    amax = np.abs(blocks).max(-1, keepdims=True)
    byte = np.maximum(np.where(amax > 0, np.frexp(amax)[1] - 1 + 127, 0) - down, 1)
    scale = np.exp2(byte - 127.0)
    codes = (blocks / scale).astype(np.float32).astype(dtype).astype(np.float64)
    return np.moveaxis((codes * scale).reshape(v.shape), -1, axis)


WIDE = False


def mx_kscale(k):
    if not WIDE:
        return np.ones(k)
    levels = np.array([10, -10, 5, -5, 0])
    if k % 512:
        return np.exp2(np.random.permutation(np.resize(levels, k // 32))).repeat(32)
    a = np.empty((k // 512, 16))
    for p in range(k // 512):
        a[p, :8] = np.random.permutation(np.resize(levels, 8))
        for g in range(8):
            far = levels[np.abs(levels - a[p, g]) >= 10]
            a[p, g + 8] = far[np.random.randint(len(far))]
    return np.exp2(a.ravel()).repeat(32)


def f64(x):
    return np.asarray(x).astype(np.float64)


def striped(idx):
    return np.tile(idx.reshape(-1, 16).T, (8, 1)).astype(np.uint16)


def unstriped(offs):
    return offs[:16].T.reshape(-1).astype(np.int64)


E2M1 = np.array([0.0, 0.5, 1.0, 1.5, 2.0, 3.0, 4.0, 6.0, -0.0, -0.5, -1.0, -1.5, -2.0, -3.0, -4.0, -6.0])


def pack_weight(w, fmt):
    k, n = w.shape
    w = f64(np.asarray(w, np.float32).astype(ml_dtypes.bfloat16)).reshape(k // 32, 32, n)
    amax = np.abs(w).max(1)
    if fmt == "e4m3":
        byte = np.frexp(amax)[1] - 1 + 127 - 7
    else:
        mant, ex = np.frexp(amax / 6.0)
        byte = np.where(mant > 0.5, ex, ex - 1) + 127
    byte = np.clip(np.where(amax > 0, byte, 1), 1, 254)
    scaled = (w * np.exp2(127.0 - byte)[:, None, :]).reshape(k, n).astype(np.float32)
    by_word = np.ascontiguousarray(scaled.reshape(k // 512, 128, 4, n).transpose(0, 1, 3, 2))
    if fmt == "e4m3":
        words = by_word.astype(ml_dtypes.float8_e4m3fn).view(np.uint8)
    else:
        c = by_word.astype(ml_dtypes.float4_e2m1fn).view(np.uint8) & 0xF
        words = (c[..., 0::2] | (c[..., 1::2] << 4)).reshape(k // 512, 128, 2 * n)
    return np.ascontiguousarray(words), np.ascontiguousarray(byte.astype(np.uint8).reshape(k // 512, 16, n))


def unpack_weight(words, scales, fmt):
    g, _, n = scales.shape
    words = np.ascontiguousarray(words).reshape(g, 128, n, -1)
    if fmt == "e4m3":
        vals = words.view(ml_dtypes.float8_e4m3fn).astype(np.float64)
    else:
        nib = np.empty((g, 128, n, 4), np.uint8)
        nib[..., 0::2] = words & 0xF
        nib[..., 1::2] = words >> 4
        vals = E2M1[nib]
    vals = vals * np.repeat(np.exp2(scales.astype(np.float64) - 127.0), 8, axis=1)[..., None]
    return vals.transpose(0, 1, 3, 2).reshape(g * 512, n)


def relu2(v):
    return np.maximum(v, 0.0) ** 2


K, T, E1, C1, E2, C2, H = 1536, 512, 8, 128, 8, 128, 512
N = 128


def deal(E, C):
    first = np.random.permutation(np.repeat(np.arange(E), T // E))
    second = (first + 1 + np.random.permutation(np.repeat(np.arange(E - 1), -(-T // (E - 1)))[:T])) % E
    while np.bincount(second, minlength=E).max() != T // E:
        load = np.bincount(second, minlength=E); hi, lo = int(load.argmax()), int(load.argmin())
        t = np.flatnonzero((second == hi) & (first != lo))[0]; second[t] = lo
    slot_token = np.empty(E * C, np.int64); pos = np.empty((2, T), np.int64); fill = np.zeros(E, np.int64)
    place = np.stack([np.random.permutation(C) for _ in range(E)])
    for r, deal in enumerate((first, second)):
        for t in np.random.permutation(T):
            e = deal[t]; j = e * C + place[e, fill[e]]; fill[e] += 1; slot_token[j] = t; pos[r, t] = j
    g = np.random.uniform(0.2, 0.8, T)
    return slot_token, pos, np.stack([g, 1.0 - g])


def by_expert(wq, xq, E, C):
    return np.concatenate([wq[e].T @ xq[:, e * C:(e + 1) * C] for e in range(E)], axis=1)


def setup_inputs():
    n = np.random.standard_normal
    s = mx_kscale(K)
    u = mx_kscale(H)
    slots1, pos1, g1 = deal(E1, C1)
    slots2, pos2, g2 = deal(E2, C2)
    x = pack_weight(n((K, T)) * s[:, None], "e4m3")
    w1 = [pack_weight(m, "e2m1") for m in n((E1, K, H)) / np.sqrt(K) / s[None, :, None] * u]
    w2 = [pack_weight(m, "e4m3") for m in n((E2, H, N)) / np.sqrt(H) / u[None, :, None] ** 2]
    return {
        "x_words": x[0],
        "x_scales": x[1],
        "w1_words": np.stack([m[0] for m in w1]),
        "w1_scales": np.stack([m[1] for m in w1]),
        "w2_words": np.stack([m[0] for m in w2]),
        "w2_scales": np.stack([m[1] for m in w2]),
        "gate1": (np.stack([np.tile(r, (128, 1)) for r in g1])).astype(np.float32),
        "gate2": (np.stack([np.tile(r, (128, 1)) for r in g2])).astype(np.float32),
        "offs": striped(slots1),
        "pos1": striped(pos1[0]),
        "pos2": striped(pos1[1]),
        "offs2": striped(slots2),
        "pos3": striped(pos2[0]),
        "pos4": striped(pos2[1]),
    }


def reference(x_words, x_scales, w1_words, w1_scales, w2_words, w2_scales, gate1, gate2, offs, pos1, pos2, offs2, pos3, pos4):
    w1 = np.stack([unpack_weight(w1_words[e], w1_scales[e], "e2m1") for e in range(E1)])
    w2 = np.stack([unpack_weight(w2_words[e], w2_scales[e], "e4m3") for e in range(E2)])
    idx, idx2 = unstriped(offs), unstriped(offs2)
    xq = unpack_weight(x_words, x_scales, "e4m3")[:, idx]
    h = relu2(by_expert(w1, xq, E1, C1))
    c = sum(f64(gate1[r, :1]) * h[:, unstriped(p)] for r, p in enumerate((pos1, pos2)))
    y = by_expert(w2, mxq(c[:, idx2], 0, "e4m3"), E2, C2)
    out = sum(f64(gate2[r, :1]) * y[:, unstriped(p)] for r, p in enumerate((pos3, pos4)))
    return out

@@ -1,0 +1,209 @@
+from contextlib import ExitStack
+
+import concourse.mybir as mybir
+from concourse.masks import make_identity
+
+K, T, E, C, H, N = 1536, 512, 8, 128, 512, 128
+S = E * C
+P = 128
+PACK = 4
+PASSES = K // (P * PACK)
+FLOPS = 2 * S * (K * H + H * N)
+
+F32 = mybir.dt.float32
+BF16 = mybir.dt.bfloat16
+I32 = mybir.dt.int32
+U32 = mybir.dt.uint32
+U16 = mybir.dt.uint16
+U8 = mybir.dt.uint8
+FP8X4 = mybir.dt.float8_e4m3fn_x4
+FP4X4 = mybir.dt.float4_e2m1fn_x4
+ACT = mybir.ActivationFunctionType
+MULT = mybir.AluOpType.mult
+ADD = mybir.AluOpType.add
+
+X_GROUPS = ((0, 3), (3, 6), (6, 7), (7, 8))
+C_GROUPS = ((0, 2), (2, 4), (4, 6), (6, 8))
+
+
+def cols(first, last, width):
+    return slice(first * width, last * width)
+
+
+def tile_moe_ser_relu2_kernel(
+    tc, x_words, x_scales, w1_words, w1_scales, w2_words, w2_scales, gate1, gate2, offs, pos1, pos2, offs2, pos3, pos4, out
+):
+    nc = tc.nc
+    with ExitStack() as ctx:
+        keep = ctx.enter_context(tc.tile_pool(name="keep", bufs=1))
+        psum = ctx.enter_context(tc.psum_pool(name="psum", bufs=4))
+
+        def load_list(name, dram):
+            tile = keep.tile(list(dram.shape), U16, name=name)
+            nc.sync.dma_start(tile[:], dram)
+            return tile
+
+        def load_scales(plane, dram):
+            rows = dram.rearrange("g (q r) n -> r q g n", r=4)
+            for r in range(4):
+                nc.sync.dma_start(plane[r:P:32].bitcast(I32), rows[r].bitcast(I32))
+
+        xs = keep.tile([P, PASSES, T], U8, align_bytes=64)
+        w1s = keep.tile([P, E * PASSES, H], U8, align_bytes=64)
+        w2s = keep.tile([P, E, N], U8, align_bytes=64)
+        half = E * PASSES // 2
+        nc.gpsimd.memset(xs[:].bitcast(I32), 0)
+        nc.vector.memset(w1s[:, :half].bitcast(I32), 0)
+        nc.vector.memset(w1s[:, half:].bitcast(I32), 0)
+        nc.vector.memset(w2s[:].bitcast(I32), 0)
+        ident = keep.tile([P, P], F32)
+        make_identity(nc, ident[:])
+
+        offs_t = load_list("offs_t", offs)
+        xw = [keep.tile([P, T], I32, name=f"xw{s}") for s in range(PASSES)]
+        for s in range(PASSES):
+            nc.sync.dma_start(xw[s][:], x_words[s].rearrange("p t d -> p (t d)").bitcast(I32))
+            if s == 0:
+                load_scales(xs, x_scales)
+        w1 = [keep.tile([P, PASSES, 2 * H], U8, name=f"w1_{e}", align_bytes=64) for e in range(E)]
+        w1_scale_rows = w1_scales.rearrange("e s b i -> (e s) b i")
+        for g in range(2):
+            load_scales(w1s[:, cols(g, g + 1, half)], w1_scale_rows[cols(g, g + 1, half)])
+            for e in range(g * E // 2, (g + 1) * E // 2):
+                nc.sync.dma_start(w1[e][:].bitcast(I32), w1_words[e].rearrange("s p n -> p s n").bitcast(I32))
+        pos1_t = load_list("pos1_t", pos1)
+        pos2_t = load_list("pos2_t", pos2)
+        g1 = [keep.tile([P, T], F32, name=f"g1_{r}") for r in range(2)]
+        for r in range(2):
+            nc.sync.dma_start(g1[r][:], gate1[r])
+        offs2_t = load_list("offs2_t", offs2)
+        w2 = keep.tile([P, E, N], I32, align_bytes=64)
+        nc.sync.dma_start(w2[:], w2_words.rearrange("f s p n d -> p (f s) (n d)").bitcast(I32))
+        load_scales(w2s, w2_scales.rearrange("f s b n -> (f s) b n"))
+        pos3_t = load_list("pos3_t", pos3)
+        pos4_t = load_list("pos4_t", pos4)
+        g2 = [keep.tile([P, T], F32, name=f"g2_{r}") for r in range(2)]
+        for r in range(2):
+            nc.sync.dma_start(g2[r][:], gate2[r])
+
+        xw_g = keep.tile([P, PASSES, S], U32, align_bytes=64)
+        xs_g = keep.tile([P, PASSES, S], U8, align_bytes=64)
+        relu = [keep.tile([P, PACK, P], F32, name=f"relu{e}") for e in range(E)]
+        h = [keep.tile([P, S], F32, name=f"h{t}") for t in range(PACK)]
+
+        def turn(t, first, last):
+            bank = psum.tile([P, 4 * C], F32, name="turned")
+            for e in range(first, last):
+                nc.tensor.transpose(bank[:, cols(e - first, e - first + 1, C)], relu[e][:, t, :], ident[:])
+            nc.scalar.activation(h[t][:, cols(first, last, C)], bank[:, cols(0, last - first, C)], ACT.Square)
+
+        for first, last in X_GROUPS:
+            offsets = offs_t[:, cols(first, last, C // 16)]
+            slots = cols(first, last, C)
+            for s in range(PASSES):
+                nc.vector.tensor_copy(xw_g[:, s, slots], xw[s][:].bitcast(U32).indirect(offsets))
+                nc.vector.tensor_copy(xs_g[:, s, slots], xs[:, s, :].indirect(offsets))
+            for e in range(first, last):
+                acc = psum.tile([P, H], F32, name="acc")
+                for s in range(PASSES):
+                    nc.tensor.matmul_mx(
+                        out=acc[:],
+                        lhsT=xw_g[:, s, cols(e, e + 1, C)].bitcast(FP8X4),
+                        lhsT_scale=xs_g[:, s, cols(e, e + 1, C)],
+                        rhs=w1[e][:, s, :].bitcast(FP4X4),
+                        rhs_scale=w1s[:, e * PASSES + s, :],
+                        start=(s == 0),
+                        stop=(s == PASSES - 1),
+                    )
+                by_plane = acc[:].rearrange("p (m t) -> p t m", t=PACK)
+                if e < E - 1:
+                    nc.scalar.activation(relu[e][:], by_plane, ACT.Relu)
+                else:
+                    nc.scalar.activation(relu[e][:, 0, :], by_plane[:, 0, :], ACT.Relu)
+                    turn(0, e, e + 1)
+                    nc.scalar.activation(relu[e][:, 1:, :], by_plane[:, 1:, :], ACT.Relu)
+                if e == 3:
+                    turn(0, 0, 4)
+                if e == 6:
+                    turn(0, 4, 7)
+        for t in range(1, PACK):
+            turn(t, 0, 4)
+            turn(t, 4, 8)
+
+        ga = keep.tile([P, PACK, T], F32)
+        gb = keep.tile([P, PACK, T], F32)
+        c_plane = [keep.tile([P, T], BF16, name=f"c{t}") for t in range(2)]
+        c_pair = keep.tile([P, T, 2], BF16)
+        cq = keep.tile([P, S, PACK], BF16, align_bytes=64)
+
+        def gated(dst, window, offsets, gate):
+            nc.vector.tensor_tensor(dst, window[:].indirect(offsets), gate, MULT)
+
+        def plane_add(t):
+            nc.vector.tensor_tensor(c_plane[t][:], ga[:, t, :], gb[:, t, :], ADD)
+            for e in range(E):
+                nc.scalar.activation(
+                    cq[:, cols(e, e + 1, C), t], c_plane[t][:].indirect(offs2_t[:, cols(e, e + 1, C // 16)]), ACT.Copy
+                )
+
+        for t in range(PACK):
+            gated(ga[:, t, :], h[t], pos1_t[:], g1[0][:])
+            if t in (1, 2):
+                plane_add(t - 1)
+            gated(gb[:, t, :], h[t], pos2_t[:], g1[1][:])
+        nc.vector.tensor_tensor(
+            c_pair[:], ga[:, 2:, :].rearrange("p t n -> p n t"), gb[:, 2:, :].rearrange("p t n -> p n t"), ADD
+        )
+
+        codes = keep.tile([P, S], U32, align_bytes=64)
+        scales = keep.tile([P, S], U8, align_bytes=64)
+        y = keep.tile([P, S], F32)
+        pair_words = c_pair[:].rearrange("p n t -> p (n t)").bitcast(U32)
+        cq_words = cq[:].bitcast(U32)
+
+        def gather_pairs(first, last):
+            nc.vector.tensor_copy(
+                cq_words[:, cols(first, last, C), 1], pair_words.indirect(offs2_t[:, cols(first, last, C // 16)])
+            )
+
+        def second_layer(first, last):
+            slots = cols(first, last, C)
+            nc.vector.quantize_mx(
+                out=codes[:, slots].bitcast(FP8X4), scales=scales[:, slots], in_=cq[:, slots].rearrange("p n t -> p (n t)")
+            )
+            bank = psum.tile([P, H], F32, name="acc")
+            for f in range(first, last):
+                nc.tensor.matmul_mx(
+                    out=bank[:, cols(f - first, f - first + 1, C)],
+                    lhsT=w2[:, f, :].bitcast(FP8X4),
+                    lhsT_scale=w2s[:, f, :],
+                    rhs=codes[:, cols(f, f + 1, C)].bitcast(FP8X4),
+                    rhs_scale=scales[:, cols(f, f + 1, C)],
+                    start=True,
+                    stop=True,
+                )
+            nc.scalar.copy(y[:, slots], bank[:, cols(0, last - first, C)])
+
+        gather_pairs(*C_GROUPS[0])
+        for j in range(1, len(C_GROUPS)):
+            gather_pairs(*C_GROUPS[j])
+            second_layer(*C_GROUPS[j - 1])
+        second_layer(*C_GROUPS[-1])
+
+        ya = keep.tile([P, T], F32)
+        yb = keep.tile([P, T], F32)
+        res = [keep.tile([P, T // 2], F32, name=f"res{j}") for j in range(2)]
+
+        def finish(j):
+            tokens = cols(j, j + 1, T // 2)
+            nc.vector.tensor_tensor(res[j][:], ya[:, tokens], yb[:, tokens], ADD)
+            nc.sync.dma_start(out[:, tokens], res[j][:])
+
+        for j in range(2):
+            tokens = cols(j, j + 1, T // 2)
+            entries = cols(j, j + 1, T // 32)
+            gated(ya[:, tokens], y, pos3_t[:, entries], g2[0][:, tokens])
+            if j == 1:
+                finish(0)
+            gated(yb[:, tokens], y, pos4_t[:, entries], g2[1][:, tokens])
+        finish(1)

@@ -22,7 +22,9 @@ ACT = mybir.ActivationFunctionType
 MULT = mybir.AluOpType.mult
 ADD = mybir.AluOpType.add
 
-X_GROUPS = ((0, 3), (3, 6), (6, 7), (7, 8))
+X_GROUPS = ((0, 1), (1, 2), (2, 5), (5, 7), (7, 8))
+S_GROUPS = (((0, 2),), ((2, 5), (5, 8)))
+SHIFTED = 112
 C_GROUPS = ((0, 2), (2, 4), (4, 6), (6, 8))
 
 
@@ -36,7 +38,7 @@ def tile_moe_ser_relu2_kernel(
     nc = tc.nc
     with ExitStack() as ctx:
         keep = ctx.enter_context(tc.tile_pool(name="keep", bufs=1))
-        psum = ctx.enter_context(tc.psum_pool(name="psum", bufs=4))
+        psum = ctx.enter_context(tc.psum_pool(name="psum", bufs=1))
 
         def load_list(name, dram):
             tile = keep.tile(list(dram.shape), U16, name=name)
@@ -48,87 +50,103 @@ def tile_moe_ser_relu2_kernel(
             for r in range(4):
                 nc.sync.dma_start(plane[r:P:32].bitcast(I32), rows[r].bitcast(I32))
 
-        xs = keep.tile([P, PASSES, T], U8, align_bytes=64)
+        xs = keep.tile([P, T], U8, tag="shared", align_bytes=64)
+        xs_moved = keep.tile([P, PASSES - 1, S], U8, align_bytes=64)
         w1s = keep.tile([P, E * PASSES, H], U8, align_bytes=64)
         w2s = keep.tile([P, E, N], U8, align_bytes=64)
-        half = E * PASSES // 2
         nc.gpsimd.memset(xs[:].bitcast(I32), 0)
-        nc.vector.memset(w1s[:, :half].bitcast(I32), 0)
-        nc.vector.memset(w1s[:, half:].bitcast(I32), 0)
-        nc.vector.memset(w2s[:].bitcast(I32), 0)
-        ident = keep.tile([P, P], F32)
-        make_identity(nc, ident[:])
+        nc.vector.memset(w1s[:].bitcast(I32), 0)
+        ident_bf = keep.tile([P, P], BF16)
+        make_identity(nc, ident_bf[:])
+        nc.gpsimd.memset(xs_moved[:].bitcast(I32), 0)
+        nc.gpsimd.memset(w2s[:].bitcast(I32), 0)
 
         offs_t = load_list("offs_t", offs)
-        xw = [keep.tile([P, T], I32, name=f"xw{s}") for s in range(PASSES)]
-        for s in range(PASSES):
-            nc.sync.dma_start(xw[s][:], x_words[s].rearrange("p t d -> p (t d)").bitcast(I32))
-            if s == 0:
-                load_scales(xs, x_scales)
+        for q in range(4):
+            nc.scalar.dma_start(xs[32 * q : 32 * q + 4 * PASSES].bitcast(I32), x_scales[:, 4 * q : 4 * q + 4, :].bitcast(I32))
+        ident = keep.tile([P, P], F32)
+        nc.scalar.activation(ident[:], ident_bf[:], ACT.Relu)
+        xw = keep.tile([P, PASSES, T], I32)
+        nc.sync.dma_start(xw[:], x_words.rearrange("s p t d -> p s (t d)").bitcast(I32))
+        load_scales(w1s, w1_scales.rearrange("e s b i -> (e s) b i"))
         w1 = [keep.tile([P, PASSES, 2 * H], U8, name=f"w1_{e}", align_bytes=64) for e in range(E)]
-        w1_scale_rows = w1_scales.rearrange("e s b i -> (e s) b i")
-        for g in range(2):
-            load_scales(w1s[:, cols(g, g + 1, half)], w1_scale_rows[cols(g, g + 1, half)])
-            for e in range(g * E // 2, (g + 1) * E // 2):
-                nc.sync.dma_start(w1[e][:].bitcast(I32), w1_words[e].rearrange("s p n -> p s n").bitcast(I32))
+        for e in range(E):
+            nc.sync.dma_start(w1[e][:].bitcast(I32), w1_words[e].rearrange("s p n -> p s n").bitcast(I32))
         pos1_t = load_list("pos1_t", pos1)
         pos2_t = load_list("pos2_t", pos2)
-        g1 = [keep.tile([P, T], F32, name=f"g1_{r}") for r in range(2)]
-        for r in range(2):
-            nc.sync.dma_start(g1[r][:], gate1[r])
+        g1 = keep.tile([P, 2, T], F32)
+        nc.sync.dma_start(g1[:], gate1.rearrange("r p t -> p r t"))
         offs2_t = load_list("offs2_t", offs2)
         w2 = keep.tile([P, E, N], I32, align_bytes=64)
         nc.sync.dma_start(w2[:], w2_words.rearrange("f s p n d -> p (f s) (n d)").bitcast(I32))
         load_scales(w2s, w2_scales.rearrange("f s b n -> (f s) b n"))
         pos3_t = load_list("pos3_t", pos3)
         pos4_t = load_list("pos4_t", pos4)
-        g2 = [keep.tile([P, T], F32, name=f"g2_{r}") for r in range(2)]
-        for r in range(2):
-            nc.sync.dma_start(g2[r][:], gate2[r])
+        g2 = keep.tile([P, 2, T], F32)
+        nc.sync.dma_start(g2[:], gate2.rearrange("r p t -> p r t"))
 
-        xw_g = keep.tile([P, PASSES, S], U32, align_bytes=64)
-        xs_g = keep.tile([P, PASSES, S], U8, align_bytes=64)
+        xs_g = keep.tile([P, S], U8, align_bytes=64)
         relu = [keep.tile([P, PACK, P], F32, name=f"relu{e}") for e in range(E)]
         h = [keep.tile([P, S], F32, name=f"h{t}") for t in range(PACK)]
 
-        def turn(t, first, last):
-            bank = psum.tile([P, 4 * C], F32, name="turned")
+        def bank_tile(b):
+            return psum.tile([P, H], F32, name=f"bank{b}")
+
+        def gather_words(dst, base, first, last):
+            for s in range(PASSES):
+                nc.vector.tensor_copy(
+                    dst[:, s, cols(first - base, last - base, C)],
+                    xw[:, s, :].bitcast(U32).indirect(offs_t[:, cols(first, last, C // 16)]),
+                )
+
+        def turn(t, first, last, b):
+            bank = bank_tile(b)
             for e in range(first, last):
                 nc.tensor.transpose(bank[:, cols(e - first, e - first + 1, C)], relu[e][:, t, :], ident[:])
             nc.scalar.activation(h[t][:, cols(first, last, C)], bank[:, cols(0, last - first, C)], ACT.Square)
 
-        for first, last in X_GROUPS:
-            offsets = offs_t[:, cols(first, last, C // 16)]
-            slots = cols(first, last, C)
+        early = X_GROUPS[0][1]
+        xw_early = keep.tile([P, PASSES, early * C], U32, align_bytes=64)
+        gather_words(xw_early, 0, 0, early)
+        for pieces in S_GROUPS:
+            for first, last in pieces:
+                nc.vector.tensor_copy(xs_g[:, cols(first, last, C)], xs[:].indirect(offs_t[:, cols(first, last, C // 16)]))
+            slots = cols(pieces[0][0], pieces[-1][1], C)
+            for s in range(1, PASSES):
+                nc.scalar.dma_start(
+                    xs_moved[:SHIFTED, s - 1, slots].bitcast(I32), xs_g[4 * s : 4 * s + SHIFTED, slots].bitcast(I32)
+                )
+        xw_late = keep.tile([P, PASSES, S - early * C], U32, tag="shared", align_bytes=64)
+        for first, last in X_GROUPS[1:]:
+            gather_words(xw_late, early, first, last)
+
+        for e in range(E):
+            acc = bank_tile(e % 4)
+            words = xw_early[:, :, cols(e, e + 1, C)] if e < early else xw_late[:, :, cols(e - early, e - early + 1, C)]
             for s in range(PASSES):
-                nc.vector.tensor_copy(xw_g[:, s, slots], xw[s][:].bitcast(U32).indirect(offsets))
-                nc.vector.tensor_copy(xs_g[:, s, slots], xs[:, s, :].indirect(offsets))
-            for e in range(first, last):
-                acc = psum.tile([P, H], F32, name="acc")
-                for s in range(PASSES):
-                    nc.tensor.matmul_mx(
-                        out=acc[:],
-                        lhsT=xw_g[:, s, cols(e, e + 1, C)].bitcast(FP8X4),
-                        lhsT_scale=xs_g[:, s, cols(e, e + 1, C)],
-                        rhs=w1[e][:, s, :].bitcast(FP4X4),
-                        rhs_scale=w1s[:, e * PASSES + s, :],
-                        start=(s == 0),
-                        stop=(s == PASSES - 1),
-                    )
-                by_plane = acc[:].rearrange("p (m t) -> p t m", t=PACK)
-                if e < E - 1:
-                    nc.scalar.activation(relu[e][:], by_plane, ACT.Relu)
-                else:
-                    nc.scalar.activation(relu[e][:, 0, :], by_plane[:, 0, :], ACT.Relu)
-                    turn(0, e, e + 1)
-                    nc.scalar.activation(relu[e][:, 1:, :], by_plane[:, 1:, :], ACT.Relu)
-                if e == 3:
-                    turn(0, 0, 4)
-                if e == 6:
-                    turn(0, 4, 7)
+                nc.tensor.matmul_mx(
+                    out=acc[:],
+                    lhsT=words[:, s, :].bitcast(FP8X4),
+                    lhsT_scale=xs_g[:, cols(e, e + 1, C)] if s == 0 else xs_moved[:, s - 1, cols(e, e + 1, C)],
+                    rhs=w1[e][:, s, :].bitcast(FP4X4),
+                    rhs_scale=w1s[:, e * PASSES + s, :],
+                    start=(s == 0),
+                    stop=(s == PASSES - 1),
+                )
+            by_plane = acc[:].rearrange("p (m t) -> p t m", t=PACK)
+            if e < E - 1:
+                nc.scalar.activation(relu[e][:], by_plane, ACT.Relu)
+            else:
+                nc.scalar.activation(relu[e][:, 0, :], by_plane[:, 0, :], ACT.Relu)
+                turn(0, e, e + 1, 6)
+                nc.scalar.activation(relu[e][:, 1:, :], by_plane[:, 1:, :], ACT.Relu)
+            if e == 3:
+                turn(0, 0, 4, 4)
+            if e == 6:
+                turn(0, 4, 7, 5)
         for t in range(1, PACK):
-            turn(t, 0, 4)
-            turn(t, 4, 8)
+            turn(t, 0, 4, 6)
+            turn(t, 4, 8, 3)
 
         ga = keep.tile([P, PACK, T], F32)
         gb = keep.tile([P, PACK, T], F32)
@@ -147,10 +165,10 @@ def tile_moe_ser_relu2_kernel(
                 )
 
         for t in range(PACK):
-            gated(ga[:, t, :], h[t], pos1_t[:], g1[0][:])
+            gated(ga[:, t, :], h[t], pos1_t[:], g1[:, 0, :])
             if t in (1, 2):
                 plane_add(t - 1)
-            gated(gb[:, t, :], h[t], pos2_t[:], g1[1][:])
+            gated(gb[:, t, :], h[t], pos2_t[:], g1[:, 1, :])
         nc.vector.tensor_tensor(
             c_pair[:], ga[:, 2:, :].rearrange("p t n -> p n t"), gb[:, 2:, :].rearrange("p t n -> p n t"), ADD
         )
@@ -171,7 +189,7 @@ def tile_moe_ser_relu2_kernel(
             nc.vector.quantize_mx(
                 out=codes[:, slots].bitcast(FP8X4), scales=scales[:, slots], in_=cq[:, slots].rearrange("p n t -> p (n t)")
             )
-            bank = psum.tile([P, H], F32, name="acc")
+            bank = bank_tile((0, 1, 2, 7)[first // 2])
             for f in range(first, last):
                 nc.tensor.matmul_mx(
                     out=bank[:, cols(f - first, f - first + 1, C)],
@@ -202,8 +220,8 @@ def tile_moe_ser_relu2_kernel(
         for j in range(2):
             tokens = cols(j, j + 1, T // 2)
             entries = cols(j, j + 1, T // 32)
-            gated(ya[:, tokens], y, pos3_t[:, entries], g2[0][:, tokens])
+            gated(ya[:, tokens], y, pos3_t[:, entries], g2[:, 0, tokens])
             if j == 1:
                 finish(0)
-            gated(yb[:, tokens], y, pos4_t[:, entries], g2[1][:, tokens])
+            gated(yb[:, tokens], y, pos4_t[:, entries], g2[:, 1, tokens])
         finish(1)

@@ -22,10 +22,10 @@ ACT = mybir.ActivationFunctionType
 MULT = mybir.AluOpType.mult
 ADD = mybir.AluOpType.add
 
-X_GROUPS = ((0, 1), (1, 2), (2, 5), (5, 7), (7, 8))
-S_GROUPS = (((0, 2),), ((2, 5), (5, 8)))
-SHIFTED = 112
-C_GROUPS = ((0, 2), (2, 4), (4, 6), (6, 8))
+X_GROUPS = ((0, 2), (2, 4), (4, 6), (6, 7), (7, 8))
+C_GROUPS = ((0, 2), (2, 4), (4, 6), (6, 7), (7, 8))
+PAIR_PIECES = ((0, 3), (3, 6), (6, 8))
+OUT_PIECES = ((0, 3), (3, 4))
 
 
 def cols(first, last, width):
@@ -45,35 +45,33 @@ def tile_moe_ser_relu2_kernel(
             nc.sync.dma_start(tile[:], dram)
             return tile
 
-        def load_scales(plane, dram):
+        def load_scales(plane, dram, queues=(nc.sync,) * 4):
             rows = dram.rearrange("g (q r) n -> r q g n", r=4)
             for r in range(4):
-                nc.sync.dma_start(plane[r:P:32].bitcast(I32), rows[r].bitcast(I32))
+                queues[r].dma_start(plane[r:P:32].bitcast(I32), rows[r].bitcast(I32))
 
-        xs = keep.tile([P, T], U8, tag="shared", align_bytes=64)
-        xs_moved = keep.tile([P, PASSES - 1, S], U8, align_bytes=64)
+        xs = keep.tile([P, PASSES, T], U8, align_bytes=64)
         w1s = keep.tile([P, E * PASSES, H], U8, align_bytes=64)
         w2s = keep.tile([P, E, N], U8, align_bytes=64)
         nc.gpsimd.memset(xs[:].bitcast(I32), 0)
-        nc.vector.memset(w1s[:].bitcast(I32), 0)
-        ident_bf = keep.tile([P, P], BF16)
-        make_identity(nc, ident_bf[:])
-        nc.gpsimd.memset(xs_moved[:].bitcast(I32), 0)
+        half = E * PASSES // 2
+        nc.vector.memset(w1s[:, :half].bitcast(I32), 0)
+        nc.gpsimd.memset(w1s[:, half:].bitcast(I32), 0)
+        ident = keep.tile([P, P], F32)
+        make_identity(nc, ident[:])
         nc.gpsimd.memset(w2s[:].bitcast(I32), 0)
 
+        load_scales(xs, x_scales, (nc.scalar,) * 4)
+        xw = [keep.tile([P, T], I32, name=f"xw{s}") for s in range(PASSES)]
+        for s in range(PASSES):
+            nc.sync.dma_start(xw[s][:], x_words[s].rearrange("p t d -> p (t d)").bitcast(I32))
         offs_t = load_list("offs_t", offs)
-        for q in range(4):
-            nc.scalar.dma_start(xs[32 * q : 32 * q + 4 * PASSES].bitcast(I32), x_scales[:, 4 * q : 4 * q + 4, :].bitcast(I32))
-        ident = keep.tile([P, P], F32)
-        nc.scalar.activation(ident[:], ident_bf[:], ACT.Relu)
-        xw = keep.tile([P, PASSES, T], I32)
-        nc.sync.dma_start(xw[:], x_words.rearrange("s p t d -> p s (t d)").bitcast(I32))
         load_scales(w1s, w1_scales.rearrange("e s b i -> (e s) b i"))
+        pos1_t = load_list("pos1_t", pos1)
+        pos2_t = load_list("pos2_t", pos2)
         w1 = [keep.tile([P, PASSES, 2 * H], U8, name=f"w1_{e}", align_bytes=64) for e in range(E)]
         for e in range(E):
             nc.sync.dma_start(w1[e][:].bitcast(I32), w1_words[e].rearrange("s p n -> p s n").bitcast(I32))
-        pos1_t = load_list("pos1_t", pos1)
-        pos2_t = load_list("pos2_t", pos2)
         g1 = keep.tile([P, 2, T], F32)
         nc.sync.dma_start(g1[:], gate1.rearrange("r p t -> p r t"))
         offs2_t = load_list("offs2_t", offs2)
@@ -85,71 +83,58 @@ def tile_moe_ser_relu2_kernel(
         g2 = keep.tile([P, 2, T], F32)
         nc.sync.dma_start(g2[:], gate2.rearrange("r p t -> p r t"))
 
-        xs_g = keep.tile([P, S], U8, align_bytes=64)
+        xw_g = keep.tile([P, PASSES, S], U32, align_bytes=64)
+        xs_g = keep.tile([P, PASSES, S], U8, align_bytes=64)
         relu = [keep.tile([P, PACK, P], F32, name=f"relu{e}") for e in range(E)]
         h = [keep.tile([P, S], F32, name=f"h{t}") for t in range(PACK)]
 
         def bank_tile(b):
             return psum.tile([P, H], F32, name=f"bank{b}")
 
-        def gather_words(dst, base, first, last):
-            for s in range(PASSES):
-                nc.vector.tensor_copy(
-                    dst[:, s, cols(first - base, last - base, C)],
-                    xw[:, s, :].bitcast(U32).indirect(offs_t[:, cols(first, last, C // 16)]),
-                )
-
-        def turn(t, first, last, b):
+        def turn(planes, first, last, b):
             bank = bank_tile(b)
-            for e in range(first, last):
-                nc.tensor.transpose(bank[:, cols(e - first, e - first + 1, C)], relu[e][:, t, :], ident[:])
-            nc.scalar.activation(h[t][:, cols(first, last, C)], bank[:, cols(0, last - first, C)], ACT.Square)
+            n = last - first
+            for j, t in enumerate(planes):
+                for e in range(first, last):
+                    place = j * n + e - first
+                    nc.tensor.transpose(bank[:, cols(place, place + 1, C)], relu[e][:, t, :], ident[:])
+            for j, t in enumerate(planes):
+                nc.scalar.activation(h[t][:, cols(first, last, C)], bank[:, cols(j * n, (j + 1) * n, C)], ACT.Square)
 
-        early = X_GROUPS[0][1]
-        xw_early = keep.tile([P, PASSES, early * C], U32, align_bytes=64)
-        gather_words(xw_early, 0, 0, early)
-        for pieces in S_GROUPS:
-            for first, last in pieces:
-                nc.vector.tensor_copy(xs_g[:, cols(first, last, C)], xs[:].indirect(offs_t[:, cols(first, last, C // 16)]))
-            slots = cols(pieces[0][0], pieces[-1][1], C)
-            for s in range(1, PASSES):
-                nc.scalar.dma_start(
-                    xs_moved[:SHIFTED, s - 1, slots].bitcast(I32), xs_g[4 * s : 4 * s + SHIFTED, slots].bitcast(I32)
-                )
-        xw_late = keep.tile([P, PASSES, S - early * C], U32, tag="shared", align_bytes=64)
-        for first, last in X_GROUPS[1:]:
-            gather_words(xw_late, early, first, last)
-
-        for e in range(E):
-            acc = bank_tile(e % 4)
-            words = xw_early[:, :, cols(e, e + 1, C)] if e < early else xw_late[:, :, cols(e - early, e - early + 1, C)]
+        for g, (first, last) in enumerate(X_GROUPS):
+            offsets = offs_t[:, cols(first, last, C // 16)]
+            slots = cols(first, last, C)
             for s in range(PASSES):
-                nc.tensor.matmul_mx(
-                    out=acc[:],
-                    lhsT=words[:, s, :].bitcast(FP8X4),
-                    lhsT_scale=xs_g[:, cols(e, e + 1, C)] if s == 0 else xs_moved[:, s - 1, cols(e, e + 1, C)],
-                    rhs=w1[e][:, s, :].bitcast(FP4X4),
-                    rhs_scale=w1s[:, e * PASSES + s, :],
-                    start=(s == 0),
-                    stop=(s == PASSES - 1),
-                )
-            by_plane = acc[:].rearrange("p (m t) -> p t m", t=PACK)
-            if e < E - 1:
-                nc.scalar.activation(relu[e][:], by_plane, ACT.Relu)
+                nc.vector.tensor_copy(xs_g[:, s, slots], xs[:, s, :].indirect(offsets))
+                nc.vector.tensor_copy(xw_g[:, s, slots], xw[s][:].bitcast(U32).indirect(offsets))
+            acc = {e: bank_tile(e % 4) for e in range(first, last)}
+            for s in range(PASSES):
+                for e in range(first, last):
+                    nc.tensor.matmul_mx(
+                        out=acc[e][:],
+                        lhsT=xw_g[:, s, cols(e, e + 1, C)].bitcast(FP8X4),
+                        lhsT_scale=xs_g[:, s, cols(e, e + 1, C)],
+                        rhs=w1[e][:, s, :].bitcast(FP4X4),
+                        rhs_scale=w1s[:, e * PASSES + s, :],
+                        start=(s == 0),
+                        stop=(s == PASSES - 1),
+                    )
+            for e in range(first, last):
+                by_plane = acc[e][:].rearrange("p (m t) -> p t m", t=PACK)
+                if e < E - 1:
+                    nc.scalar.activation(relu[e][:], by_plane, ACT.Relu)
+                else:
+                    nc.scalar.activation(relu[e][:, 0, :], by_plane[:, 0, :], ACT.Relu)
+                    nc.scalar.activation(relu[e][:, 1:, :], by_plane[:, 1:, :], ACT.Relu)
+            if last - first == 2:
+                turn((0, 1), first, last, 4 + 2 * (g % 2))
+                turn((2, 3), first, last, 5 + 2 * (g % 2))
+            elif last < E:
+                turn((0, 1, 2, 3), first, last, 6)
             else:
-                nc.scalar.activation(relu[e][:, 0, :], by_plane[:, 0, :], ACT.Relu)
-                turn(0, e, e + 1, 6)
-                nc.scalar.activation(relu[e][:, 1:, :], by_plane[:, 1:, :], ACT.Relu)
-            if e == 3:
-                turn(0, 0, 4, 4)
-            if e == 6:
-                turn(0, 4, 7, 5)
-        for t in range(1, PACK):
-            turn(t, 0, 4, 6)
-            turn(t, 4, 8, 3)
+                turn((0,), first, last, 7)
+                turn((1, 2, 3), first, last, 4)
 
-        ga = keep.tile([P, PACK, T], F32)
-        gb = keep.tile([P, PACK, T], F32)
         c_plane = [keep.tile([P, T], BF16, name=f"c{t}") for t in range(2)]
         c_pair = keep.tile([P, T, 2], BF16)
         cq = keep.tile([P, S, PACK], BF16, align_bytes=64)
@@ -157,21 +142,22 @@ def tile_moe_ser_relu2_kernel(
         def gated(dst, window, offsets, gate):
             nc.vector.tensor_tensor(dst, window[:].indirect(offsets), gate, MULT)
 
-        def plane_add(t):
-            nc.vector.tensor_tensor(c_plane[t][:], ga[:, t, :], gb[:, t, :], ADD)
+        for t in range(2):
+            ga = keep.tile([P, T], F32, name=f"ga{t}")
+            gb = keep.tile([P, T], F32, name=f"gb{t}")
+            gated(ga[:], h[t], pos1_t[:], g1[:, 0, :])
+            gated(gb[:], h[t], pos2_t[:], g1[:, 1, :])
+            nc.vector.tensor_tensor(c_plane[t][:], ga[:], gb[:], ADD)
             for e in range(E):
                 nc.scalar.activation(
                     cq[:, cols(e, e + 1, C), t], c_plane[t][:].indirect(offs2_t[:, cols(e, e + 1, C // 16)]), ACT.Copy
                 )
-
-        for t in range(PACK):
-            gated(ga[:, t, :], h[t], pos1_t[:], g1[:, 0, :])
-            if t in (1, 2):
-                plane_add(t - 1)
-            gated(gb[:, t, :], h[t], pos2_t[:], g1[:, 1, :])
-        nc.vector.tensor_tensor(
-            c_pair[:], ga[:, 2:, :].rearrange("p t n -> p n t"), gb[:, 2:, :].rearrange("p t n -> p n t"), ADD
-        )
+        ga_pair = keep.tile([P, 2, T], F32, tag="ga0")
+        gb_pair = keep.tile([P, 2, T], F32, tag="gb0")
+        for j in range(2):
+            gated(ga_pair[:, j, :], h[2 + j], pos1_t[:], g1[:, 0, :])
+            gated(gb_pair[:, j, :], h[2 + j], pos2_t[:], g1[:, 1, :])
+        nc.vector.tensor_tensor(c_pair[:], ga_pair[:].rearrange("p t n -> p n t"), gb_pair[:].rearrange("p t n -> p n t"), ADD)
 
         codes = keep.tile([P, S], U32, align_bytes=64)
         scales = keep.tile([P, S], U8, align_bytes=64)
@@ -189,7 +175,7 @@ def tile_moe_ser_relu2_kernel(
             nc.vector.quantize_mx(
                 out=codes[:, slots].bitcast(FP8X4), scales=scales[:, slots], in_=cq[:, slots].rearrange("p n t -> p (n t)")
             )
-            bank = bank_tile((0, 1, 2, 7)[first // 2])
+            bank = bank_tile((0, 1, 2, 3, 5)[C_GROUPS.index((first, last))])
             for f in range(first, last):
                 nc.tensor.matmul_mx(
                     out=bank[:, cols(f - first, f - first + 1, C)],
@@ -202,26 +188,25 @@ def tile_moe_ser_relu2_kernel(
                 )
             nc.scalar.copy(y[:, slots], bank[:, cols(0, last - first, C)])
 
-        gather_pairs(*C_GROUPS[0])
-        for j in range(1, len(C_GROUPS)):
-            gather_pairs(*C_GROUPS[j])
-            second_layer(*C_GROUPS[j - 1])
-        second_layer(*C_GROUPS[-1])
+        for first, last in PAIR_PIECES:
+            gather_pairs(first, last)
+        for first, last in C_GROUPS:
+            second_layer(first, last)
 
         ya = keep.tile([P, T], F32)
         yb = keep.tile([P, T], F32)
-        res = [keep.tile([P, T // 2], F32, name=f"res{j}") for j in range(2)]
+        res = keep.tile([P, T], F32)
 
-        def finish(j):
-            tokens = cols(j, j + 1, T // 2)
-            nc.vector.tensor_tensor(res[j][:], ya[:, tokens], yb[:, tokens], ADD)
-            nc.sync.dma_start(out[:, tokens], res[j][:])
+        def finish(first, last):
+            tokens = cols(first, last, P)
+            nc.vector.tensor_tensor(res[:, tokens], ya[:, tokens], yb[:, tokens], ADD)
+            nc.sync.dma_start(out[:, tokens], res[:, tokens])
 
-        for j in range(2):
-            tokens = cols(j, j + 1, T // 2)
-            entries = cols(j, j + 1, T // 32)
+        for j, (first, last) in enumerate(OUT_PIECES):
+            tokens = cols(first, last, P)
+            entries = cols(first, last, P // 16)
             gated(ya[:, tokens], y, pos3_t[:, entries], g2[:, 0, tokens])
-            if j == 1:
-                finish(0)
+            if j > 0:
+                finish(*OUT_PIECES[j - 1])
             gated(yb[:, tokens], y, pos4_t[:, entries], g2[:, 1, tokens])
-        finish(1)
+        finish(*OUT_PIECES[-1])

@@ -22,7 +22,9 @@ ACT = mybir.ActivationFunctionType
 MULT = mybir.AluOpType.mult
 ADD = mybir.AluOpType.add
 
-X_GROUPS = ((0, 2), (2, 4), (4, 6), (6, 7), (7, 8))
+X_GROUPS = ((0, 2), (2, 5), (5, 7), (7, 8))
+S_GROUPS = (((0, 2),), ((2, 5), (5, 8)))
+SHIFTED = 112
 C_GROUPS = ((0, 2), (2, 4), (4, 6), (6, 7), (7, 8))
 PAIR_PIECES = ((0, 3), (3, 6), (6, 8))
 OUT_PIECES = ((0, 3), (3, 4))
@@ -45,33 +47,38 @@ def tile_moe_ser_relu2_kernel(
             nc.sync.dma_start(tile[:], dram)
             return tile
 
-        def load_scales(plane, dram, queues=(nc.sync,) * 4):
+        def load_scales(plane, dram, queues=(nc.sync, nc.sync)):
             rows = dram.rearrange("g (q r) n -> r q g n", r=4)
             for r in range(4):
-                queues[r].dma_start(plane[r:P:32].bitcast(I32), rows[r].bitcast(I32))
+                queues[r % 2].dma_start(plane[r:P:32].bitcast(I32), rows[r].bitcast(I32))
 
-        xs = keep.tile([P, PASSES, T], U8, align_bytes=64)
+        xs = keep.tile([P, T], U8, tag="shared", align_bytes=64)
+        xs_moved = keep.tile([P, PASSES - 1, S], U8, align_bytes=64)
         w1s = keep.tile([P, E * PASSES, H], U8, align_bytes=64)
         w2s = keep.tile([P, E, N], U8, align_bytes=64)
         nc.gpsimd.memset(xs[:].bitcast(I32), 0)
         half = E * PASSES // 2
         nc.vector.memset(w1s[:, :half].bitcast(I32), 0)
+        nc.vector.memset(xs_moved[:].bitcast(I32), 0)
         nc.gpsimd.memset(w1s[:, half:].bitcast(I32), 0)
         ident = keep.tile([P, P], F32)
         make_identity(nc, ident[:])
         nc.gpsimd.memset(w2s[:].bitcast(I32), 0)
 
-        load_scales(xs, x_scales, (nc.scalar,) * 4)
+        offs_t = load_list("offs_t", offs)
         xw = [keep.tile([P, T], I32, name=f"xw{s}") for s in range(PASSES)]
         for s in range(PASSES):
             nc.sync.dma_start(xw[s][:], x_words[s].rearrange("p t d -> p (t d)").bitcast(I32))
-        offs_t = load_list("offs_t", offs)
-        load_scales(w1s, w1_scales.rearrange("e s b i -> (e s) b i"))
-        pos1_t = load_list("pos1_t", pos1)
-        pos2_t = load_list("pos2_t", pos2)
+        for q in range(4):
+            nc.scalar.dma_start(xs[32 * q : 32 * q + 4 * PASSES].bitcast(I32), x_scales[:, 4 * q : 4 * q + 4, :].bitcast(I32))
+        w1_scale_rows = w1_scales.rearrange("e s b i -> (e s) b i")
+        for j in range(3):
+            load_scales(w1s[:, cols(j, j + 1, E)], w1_scale_rows[cols(j, j + 1, E)], (nc.sync, nc.scalar))
         w1 = [keep.tile([P, PASSES, 2 * H], U8, name=f"w1_{e}", align_bytes=64) for e in range(E)]
         for e in range(E):
             nc.sync.dma_start(w1[e][:].bitcast(I32), w1_words[e].rearrange("s p n -> p s n").bitcast(I32))
+        pos1_t = load_list("pos1_t", pos1)
+        pos2_t = load_list("pos2_t", pos2)
         g1 = keep.tile([P, 2, T], F32)
         nc.sync.dma_start(g1[:], gate1.rearrange("r p t -> p r t"))
         offs2_t = load_list("offs2_t", offs2)
@@ -83,57 +90,68 @@ def tile_moe_ser_relu2_kernel(
         g2 = keep.tile([P, 2, T], F32)
         nc.sync.dma_start(g2[:], gate2.rearrange("r p t -> p r t"))
 
-        xw_g = keep.tile([P, PASSES, S], U32, align_bytes=64)
-        xs_g = keep.tile([P, PASSES, S], U8, align_bytes=64)
+        xs_g = keep.tile([P, S], U8, align_bytes=64)
         relu = [keep.tile([P, PACK, P], F32, name=f"relu{e}") for e in range(E)]
         h = [keep.tile([P, S], F32, name=f"h{t}") for t in range(PACK)]
 
         def bank_tile(b):
             return psum.tile([P, H], F32, name=f"bank{b}")
 
-        def turn(planes, first, last, b):
-            bank = bank_tile(b)
-            n = last - first
-            for j, t in enumerate(planes):
-                for e in range(first, last):
-                    place = j * n + e - first
-                    nc.tensor.transpose(bank[:, cols(place, place + 1, C)], relu[e][:, t, :], ident[:])
-            for j, t in enumerate(planes):
-                nc.scalar.activation(h[t][:, cols(first, last, C)], bank[:, cols(j * n, (j + 1) * n, C)], ACT.Square)
+        def gather_words(dst, base, first, last):
+            for s in range(PASSES):
+                nc.vector.tensor_copy(
+                    dst[:, s, cols(first - base, last - base, C)],
+                    xw[s][:].bitcast(U32).indirect(offs_t[:, cols(first, last, C // 16)]),
+                )
 
-        for g, (first, last) in enumerate(X_GROUPS):
-            offsets = offs_t[:, cols(first, last, C // 16)]
-            slots = cols(first, last, C)
-            for s in range(PASSES):
-                nc.vector.tensor_copy(xs_g[:, s, slots], xs[:, s, :].indirect(offsets))
-                nc.vector.tensor_copy(xw_g[:, s, slots], xw[s][:].bitcast(U32).indirect(offsets))
-            acc = {e: bank_tile(e % 4) for e in range(first, last)}
-            for s in range(PASSES):
-                for e in range(first, last):
-                    nc.tensor.matmul_mx(
-                        out=acc[e][:],
-                        lhsT=xw_g[:, s, cols(e, e + 1, C)].bitcast(FP8X4),
-                        lhsT_scale=xs_g[:, s, cols(e, e + 1, C)],
-                        rhs=w1[e][:, s, :].bitcast(FP4X4),
-                        rhs_scale=w1s[:, e * PASSES + s, :],
-                        start=(s == 0),
-                        stop=(s == PASSES - 1),
-                    )
+        def turn(t, first, last, b):
+            bank = bank_tile(b)
             for e in range(first, last):
-                by_plane = acc[e][:].rearrange("p (m t) -> p t m", t=PACK)
-                if e < E - 1:
-                    nc.scalar.activation(relu[e][:], by_plane, ACT.Relu)
-                else:
-                    nc.scalar.activation(relu[e][:, 0, :], by_plane[:, 0, :], ACT.Relu)
-                    nc.scalar.activation(relu[e][:, 1:, :], by_plane[:, 1:, :], ACT.Relu)
-            if last - first == 2:
-                turn((0, 1), first, last, 4 + 2 * (g % 2))
-                turn((2, 3), first, last, 5 + 2 * (g % 2))
-            elif last < E:
-                turn((0, 1, 2, 3), first, last, 6)
+                nc.tensor.transpose(bank[:, cols(e - first, e - first + 1, C)], relu[e][:, t, :], ident[:])
+            nc.scalar.activation(h[t][:, cols(first, last, C)], bank[:, cols(0, last - first, C)], ACT.Square)
+
+        early = X_GROUPS[0][1]
+        xw_early = keep.tile([P, PASSES, early * C], U32, align_bytes=64)
+        gather_words(xw_early, 0, 0, early)
+        for pieces in S_GROUPS:
+            for first, last in pieces:
+                nc.vector.tensor_copy(xs_g[:, cols(first, last, C)], xs[:].indirect(offs_t[:, cols(first, last, C // 16)]))
+            slots = cols(pieces[0][0], pieces[-1][1], C)
+            for s in range(1, PASSES):
+                nc.scalar.dma_start(
+                    xs_moved[:SHIFTED, s - 1, slots].bitcast(I32), xs_g[4 * s : 4 * s + SHIFTED, slots].bitcast(I32)
+                )
+        xw_late = keep.tile([P, PASSES, S - early * C], U32, tag="shared", align_bytes=64)
+        for first, last in X_GROUPS[1:]:
+            gather_words(xw_late, early, first, last)
+
+        for e in range(E):
+            acc = bank_tile(e % 4)
+            words = xw_early[:, :, cols(e, e + 1, C)] if e < early else xw_late[:, :, cols(e - early, e - early + 1, C)]
+            for s in range(PASSES):
+                nc.tensor.matmul_mx(
+                    out=acc[:],
+                    lhsT=words[:, s, :].bitcast(FP8X4),
+                    lhsT_scale=xs_g[:, cols(e, e + 1, C)] if s == 0 else xs_moved[:, s - 1, cols(e, e + 1, C)],
+                    rhs=w1[e][:, s, :].bitcast(FP4X4),
+                    rhs_scale=w1s[:, e * PASSES + s, :],
+                    start=(s == 0),
+                    stop=(s == PASSES - 1),
+                )
+            by_plane = acc[:].rearrange("p (m t) -> p t m", t=PACK)
+            if e < E - 1:
+                nc.scalar.activation(relu[e][:], by_plane, ACT.Relu)
             else:
-                turn((0,), first, last, 7)
-                turn((1, 2, 3), first, last, 4)
+                nc.scalar.activation(relu[e][:, 0, :], by_plane[:, 0, :], ACT.Relu)
+                nc.scalar.activation(relu[e][:, 1:, :], by_plane[:, 1:, :], ACT.Relu)
+                turn(0, e, e + 1, 6)
+            if e == 3:
+                turn(0, 0, 4, 4)
+            if e == 6:
+                turn(0, 4, 7, 5)
+        for t in range(1, PACK):
+            turn(t, 0, 4, 3)
+            turn(t, 4, 8, 6)
 
         c_plane = [keep.tile([P, T], BF16, name=f"c{t}") for t in range(2)]
         c_pair = keep.tile([P, T, 2], BF16)
@@ -175,7 +193,7 @@ def tile_moe_ser_relu2_kernel(
             nc.vector.quantize_mx(
                 out=codes[:, slots].bitcast(FP8X4), scales=scales[:, slots], in_=cq[:, slots].rearrange("p n t -> p (n t)")
             )
-            bank = bank_tile((0, 1, 2, 3, 5)[C_GROUPS.index((first, last))])
+            bank = bank_tile((0, 1, 2, 7, 4)[C_GROUPS.index((first, last))])
             for f in range(first, last):
                 nc.tensor.matmul_mx(
                     out=bank[:, cols(f - first, f - first + 1, C)],

@@ -155,7 +155,9 @@ def tile_moe_ser_relu2_kernel(
 
         c_plane = [keep.tile([P, T], BF16, name=f"c{t}") for t in range(2)]
         c_pair = keep.tile([P, T, 2], BF16)
-        cq = keep.tile([P, S, PACK], BF16, align_bytes=64)
+        slot_pairs = keep.tile([P, 2, S], I32)
+        low_pairs = slot_pairs[:, 0, :].bitcast(BF16).rearrange("p (n t) -> p n t", t=2)
+        cq = keep.tile([P, S, 2], I32, align_bytes=64)
 
         def gated(dst, window, offsets, gate):
             nc.vector.tensor_tensor(dst, window[:].indirect(offsets), gate, MULT)
@@ -168,7 +170,7 @@ def tile_moe_ser_relu2_kernel(
             nc.vector.tensor_tensor(c_plane[t][:], ga[:], gb[:], ADD)
             for e in range(E):
                 nc.scalar.activation(
-                    cq[:, cols(e, e + 1, C), t], c_plane[t][:].indirect(offs2_t[:, cols(e, e + 1, C // 16)]), ACT.Copy
+                    low_pairs[:, cols(e, e + 1, C), t], c_plane[t][:].indirect(offs2_t[:, cols(e, e + 1, C // 16)]), ACT.Copy
                 )
         ga_pair = keep.tile([P, 2, T], F32, tag="ga0")
         gb_pair = keep.tile([P, 2, T], F32, tag="gb0")
@@ -181,17 +183,16 @@ def tile_moe_ser_relu2_kernel(
         scales = keep.tile([P, S], U8, align_bytes=64)
         y = keep.tile([P, S], F32)
         pair_words = c_pair[:].rearrange("p n t -> p (n t)").bitcast(U32)
-        cq_words = cq[:].bitcast(U32)
 
         def gather_pairs(first, last):
             nc.vector.tensor_copy(
-                cq_words[:, cols(first, last, C), 1], pair_words.indirect(offs2_t[:, cols(first, last, C // 16)])
+                slot_pairs[:, 1, cols(first, last, C)].bitcast(U32), pair_words.indirect(offs2_t[:, cols(first, last, C // 16)])
             )
 
         def second_layer(first, last):
             slots = cols(first, last, C)
             nc.vector.quantize_mx(
-                out=codes[:, slots].bitcast(FP8X4), scales=scales[:, slots], in_=cq[:, slots].rearrange("p n t -> p (n t)")
+                out=codes[:, slots].bitcast(FP8X4), scales=scales[:, slots], in_=cq[:, slots].rearrange("p n j -> p (n j)").bitcast(BF16)
             )
             bank = bank_tile((0, 1, 2, 7, 4)[C_GROUPS.index((first, last))])
             for f in range(first, last):
@@ -208,8 +209,12 @@ def tile_moe_ser_relu2_kernel(
 
         for first, last in PAIR_PIECES:
             gather_pairs(first, last)
-        for first, last in C_GROUPS:
-            second_layer(first, last)
+        for j, (first, last) in enumerate(C_GROUPS):
+            slots = cols(first, last, C)
+            nc.vector.tensor_copy(cq[:, slots], slot_pairs[:, :, slots].rearrange("p j n -> p n j"))
+            if j > 0:
+                second_layer(*C_GROUPS[j - 1])
+        second_layer(*C_GROUPS[-1])
 
         ya = keep.tile([P, T], F32)
         yb = keep.tile([P, T], F32)

@@ -1,7 +1,6 @@
 from contextlib import ExitStack
 
 import concourse.mybir as mybir
-from concourse.masks import make_identity
 
 K, T, E, C, H, N = 1536, 512, 8, 128, 512, 128
 S = E * C
@@ -22,8 +21,8 @@ ACT = mybir.ActivationFunctionType
 MULT = mybir.AluOpType.mult
 ADD = mybir.AluOpType.add
 
-X_GROUPS = ((0, 2), (2, 5), (5, 7), (7, 8))
-S_GROUPS = (((0, 2),), ((2, 5), (5, 8)))
+EARLY = 4
+BYTE_PIECES = ((0, 3), (3, 6), (6, 8))
 SHIFTED = 112
 C_GROUPS = ((0, 2), (2, 4), (4, 6), (6, 7), (7, 8))
 PAIR_PIECES = ((0, 3), (3, 6), (6, 8))
@@ -54,15 +53,21 @@ def tile_moe_ser_relu2_kernel(
 
         xs = keep.tile([P, T], U8, tag="shared", align_bytes=64)
         xs_moved = keep.tile([P, PASSES - 1, S], U8, align_bytes=64)
-        w1s = keep.tile([P, E * PASSES, H], U8, align_bytes=64)
+        half = E * PASSES // 2
+        w1s = [keep.tile([P, half, H], U8, name=f"w1s{j}", align_bytes=64) for j in range(2)]
         w2s = keep.tile([P, E, N], U8, align_bytes=64)
         nc.gpsimd.memset(xs[:].bitcast(I32), 0)
-        half = E * PASSES // 2
-        nc.vector.memset(w1s[:, :half].bitcast(I32), 0)
-        nc.vector.memset(xs_moved[:].bitcast(I32), 0)
-        nc.gpsimd.memset(w1s[:, half:].bitcast(I32), 0)
+        ones_raw = keep.tile([P, P], F32)
+        nc.vector.memset(ones_raw[:], 1.0)
+        nc.vector.memset(w1s[0][:].bitcast(I32), 0)
+        nc.gpsimd.memset(w1s[1][:].bitcast(I32), 0)
+        ones = keep.tile([P, P], F32)
+        nc.scalar.activation(ones[:], ones_raw[:], ACT.Relu)
         ident = keep.tile([P, P], F32)
-        make_identity(nc, ident[:])
+        nc.gpsimd.affine_select(
+            out=ident[:], in_=ones[:], compare_op=mybir.AluOpType.is_equal, fill=0.0, base=0, pattern=[[-1, P]], channel_multiplier=1
+        )
+        nc.gpsimd.memset(xs_moved[:].bitcast(I32), 0)
         nc.gpsimd.memset(w2s[:].bitcast(I32), 0)
 
         offs_t = load_list("offs_t", offs)
@@ -70,17 +75,28 @@ def tile_moe_ser_relu2_kernel(
         for s in range(PASSES):
             nc.sync.dma_start(xw[s][:], x_words[s].rearrange("p t d -> p (t d)").bitcast(I32))
         for q in range(4):
-            nc.scalar.dma_start(xs[32 * q : 32 * q + 4 * PASSES].bitcast(I32), x_scales[:, 4 * q : 4 * q + 4, :].bitcast(I32))
+            (nc.scalar if q < 2 else nc.sync).dma_start(xs[32 * q : 32 * q + 4 * PASSES].bitcast(I32), x_scales[:, 4 * q : 4 * q + 4, :].bitcast(I32))
         w1_scale_rows = w1_scales.rearrange("e s b i -> (e s) b i")
-        for j in range(3):
-            load_scales(w1s[:, cols(j, j + 1, E)], w1_scale_rows[cols(j, j + 1, E)], (nc.sync, nc.scalar))
-        w1 = [keep.tile([P, PASSES, 2 * H], U8, name=f"w1_{e}", align_bytes=64) for e in range(E)]
-        for e in range(E):
-            nc.sync.dma_start(w1[e][:].bitcast(I32), w1_words[e].rearrange("s p n -> p s n").bitcast(I32))
+        w1_rows = w1_words.rearrange("e s p n -> p (e s) n")
+        w1 = []
+
+        def load_w1(first, last):
+            tile = keep.tile([P, last - first, 2 * H], U8, name=f"w1_{first}", align_bytes=64)
+            nc.sync.dma_start(tile[:].bitcast(I32), w1_rows[:, first:last, :].bitcast(I32))
+            w1.extend(tile[:, j, :] for j in range(last - first))
+
+        load_w1(0, 6)
+        load_scales(w1s[0], w1_scale_rows[:half])
+        load_w1(6, 12)
+        load_w1(12, 18)
+        load_scales(w1s[1], w1_scale_rows[half:])
+        load_w1(18, 22)
+        load_w1(22, 24)
         pos1_t = load_list("pos1_t", pos1)
         pos2_t = load_list("pos2_t", pos2)
         g1 = keep.tile([P, 2, T], F32)
-        nc.sync.dma_start(g1[:], gate1.rearrange("r p t -> p r t"))
+        for r in range(2):
+            nc.sync.dma_start(g1[:, r, :], gate1[r])
         offs2_t = load_list("offs2_t", offs2)
         w2 = keep.tile([P, E, N], I32, align_bytes=64)
         nc.sync.dma_start(w2[:], w2_words.rearrange("f s p n d -> p (f s) (n d)").bitcast(I32))
@@ -97,12 +113,8 @@ def tile_moe_ser_relu2_kernel(
         def bank_tile(b):
             return psum.tile([P, H], F32, name=f"bank{b}")
 
-        def gather_words(dst, base, first, last):
-            for s in range(PASSES):
-                nc.vector.tensor_copy(
-                    dst[:, s, cols(first - base, last - base, C)],
-                    xw[s][:].bitcast(U32).indirect(offs_t[:, cols(first, last, C // 16)]),
-                )
+        def gather_words(dst, s, first, last):
+            nc.vector.tensor_copy(dst, xw[s][:].bitcast(U32).indirect(offs_t[:, cols(first, last, C // 16)]))
 
         def turn(t, first, last, b):
             bank = bank_tile(b)
@@ -110,45 +122,63 @@ def tile_moe_ser_relu2_kernel(
                 nc.tensor.transpose(bank[:, cols(e - first, e - first + 1, C)], relu[e][:, t, :], ident[:])
             nc.scalar.activation(h[t][:, cols(first, last, C)], bank[:, cols(0, last - first, C)], ACT.Square)
 
-        early = X_GROUPS[0][1]
-        xw_early = keep.tile([P, PASSES, early * C], U32, align_bytes=64)
-        gather_words(xw_early, 0, 0, early)
-        for pieces in S_GROUPS:
-            for first, last in pieces:
-                nc.vector.tensor_copy(xs_g[:, cols(first, last, C)], xs[:].indirect(offs_t[:, cols(first, last, C // 16)]))
-            slots = cols(pieces[0][0], pieces[-1][1], C)
-            for s in range(1, PASSES):
-                nc.scalar.dma_start(
-                    xs_moved[:SHIFTED, s - 1, slots].bitcast(I32), xs_g[4 * s : 4 * s + SHIFTED, slots].bitcast(I32)
-                )
-        xw_late = keep.tile([P, PASSES, S - early * C], U32, tag="shared", align_bytes=64)
-        for first, last in X_GROUPS[1:]:
-            gather_words(xw_late, early, first, last)
+        xw_early = keep.tile([P, EARLY * C], U32, align_bytes=64)
+        for first in range(0, EARLY, 2):
+            gather_words(xw_early[:, cols(first, first + 2, C)], 0, first, first + 2)
+        for first, last in BYTE_PIECES:
+            nc.vector.tensor_copy(xs_g[:, cols(first, last, C)], xs[:].indirect(offs_t[:, cols(first, last, C // 16)]))
+        for s in range(1, PASSES):
+            nc.scalar.dma_start(xs_moved[:SHIFTED, s - 1, :].bitcast(I32), xs_g[4 * s : 4 * s + SHIFTED, :].bitcast(I32))
+        xw_late = keep.tile([P, PASSES * S - EARLY * C], U32, tag="shared", align_bytes=64)
 
-        for e in range(E):
-            acc = bank_tile(e % 4)
-            words = xw_early[:, :, cols(e, e + 1, C)] if e < early else xw_late[:, :, cols(e - early, e - early + 1, C)]
+        def words(s, first, last):
+            if s == 0 and first < EARLY:
+                return xw_early[:, cols(first, last, C)]
+            return xw_late[:, cols(s * E - EARLY + first, s * E - EARLY + last, C)]
+
+        for first in range(0, E, 2):
             for s in range(PASSES):
-                nc.tensor.matmul_mx(
-                    out=acc[:],
-                    lhsT=words[:, s, :].bitcast(FP8X4),
-                    lhsT_scale=xs_g[:, cols(e, e + 1, C)] if s == 0 else xs_moved[:, s - 1, cols(e, e + 1, C)],
-                    rhs=w1[e][:, s, :].bitcast(FP4X4),
-                    rhs_scale=w1s[:, e * PASSES + s, :],
-                    start=(s == 0),
-                    stop=(s == PASSES - 1),
-                )
-            by_plane = acc[:].rearrange("p (m t) -> p t m", t=PACK)
+                if s > 0 or first >= EARLY:
+                    gather_words(words(s, first, first + 2), s, first, first + 2)
+
+        def one_pass(acc, e, s):
+            nc.tensor.matmul_mx(
+                out=acc[:],
+                lhsT=words(s, e, e + 1).bitcast(FP8X4),
+                lhsT_scale=xs_g[:, cols(e, e + 1, C)] if s == 0 else xs_moved[:, s - 1, cols(e, e + 1, C)],
+                rhs=w1[e * PASSES + s].bitcast(FP4X4),
+                rhs_scale=w1s[e // 4][:, e % 4 * PASSES + s, :],
+                start=(s == 0),
+                stop=(s == PASSES - 1),
+            )
+
+        def rectify(e, acc, planes):
+            by_plane = acc[:].rearrange("p (m t) -> p t m", t=PACK)[:, planes, :]
             if e < E - 1:
-                nc.scalar.activation(relu[e][:], by_plane, ACT.Relu)
+                nc.scalar.activation(relu[e][:, planes, :], by_plane, ACT.Relu)
             else:
-                nc.scalar.activation(relu[e][:, 0, :], by_plane[:, 0, :], ACT.Relu)
-                nc.scalar.activation(relu[e][:, 1:, :], by_plane[:, 1:, :], ACT.Relu)
-                turn(0, e, e + 1, 6)
+                nc.vector.tensor_scalar_max(relu[e][:, planes, :], by_plane, 0.0)
+
+        first_two = [bank_tile(e) for e in range(2)]
+        for s in range(PASSES):
+            for e in range(2):
+                one_pass(first_two[e], e, s)
+        for e in range(E):
+            if e < 2:
+                acc = first_two[e]
+            else:
+                acc = bank_tile(e % 4)
+                for s in range(PASSES):
+                    one_pass(acc, e, s)
+            if e < E - 1:
+                rectify(e, acc, slice(0, PACK))
+            else:
+                rectify(e, acc, slice(0, 1))
+                turn(0, 4, 7, 5)
+                turn(0, 7, 8, 6)
+                rectify(e, acc, slice(1, PACK))
             if e == 3:
                 turn(0, 0, 4, 4)
-            if e == 6:
-                turn(0, 4, 7, 5)
         for t in range(1, PACK):
             turn(t, 0, 4, 3)
             turn(t, 4, 8, 6)

@@ -22,7 +22,8 @@ MULT = mybir.AluOpType.mult
 ADD = mybir.AluOpType.add
 
 EARLY = 4
-BYTE_PIECES = ((0, 3), (3, 6), (6, 8))
+BYTE_GROUPS = (((0, 2),), ((2, 5), (5, 8)))
+FIRST = 2
 SHIFTED = 112
 C_GROUPS = ((0, 2), (2, 4), (4, 6), (6, 7), (7, 8))
 PAIR_PIECES = ((0, 3), (3, 6), (6, 8))
@@ -46,29 +47,24 @@ def tile_moe_ser_relu2_kernel(
             nc.sync.dma_start(tile[:], dram)
             return tile
 
-        def load_scales(plane, dram, queues=(nc.sync, nc.sync)):
+        def load_scales(plane, dram, queue=nc.sync, which=range(4)):
             rows = dram.rearrange("g (q r) n -> r q g n", r=4)
-            for r in range(4):
-                queues[r % 2].dma_start(plane[r:P:32].bitcast(I32), rows[r].bitcast(I32))
+            for r in which:
+                queue.dma_start(plane[r:P:32].bitcast(I32), rows[r].bitcast(I32))
 
-        xs = keep.tile([P, T], U8, tag="shared", align_bytes=64)
+        late = ctx.enter_context(tc.tile_pool(name="late", bufs=1))
+        late_words = PASSES * S - EARLY * C
+        xs_span = late.tile([P, 4 * late_words + (E - 2) * PASSES * 2 * H], U8, align_bytes=64, offset=0)
+        xs = xs_span[:, :T]
         xs_moved = keep.tile([P, PASSES - 1, S], U8, align_bytes=64)
-        half = E * PASSES // 2
-        w1s = [keep.tile([P, half, H], U8, name=f"w1s{j}", align_bytes=64) for j in range(2)]
+        head = FIRST * PASSES
+        w1s_head = keep.tile([P, head, H], U8, align_bytes=64)
+        w1s_rest = keep.tile([P, E * PASSES - head, H], U8, align_bytes=64)
         w2s = keep.tile([P, E, N], U8, align_bytes=64)
-        nc.gpsimd.memset(xs[:].bitcast(I32), 0)
-        ones_raw = keep.tile([P, P], F32)
-        nc.vector.memset(ones_raw[:], 1.0)
-        nc.vector.memset(w1s[0][:].bitcast(I32), 0)
-        nc.gpsimd.memset(w1s[1][:].bitcast(I32), 0)
-        ones = keep.tile([P, P], F32)
-        nc.scalar.activation(ones[:], ones_raw[:], ACT.Relu)
-        ident = keep.tile([P, P], F32)
-        nc.gpsimd.affine_select(
-            out=ident[:], in_=ones[:], compare_op=mybir.AluOpType.is_equal, fill=0.0, base=0, pattern=[[-1, P]], channel_multiplier=1
-        )
-        nc.gpsimd.memset(xs_moved[:].bitcast(I32), 0)
-        nc.gpsimd.memset(w2s[:].bitcast(I32), 0)
+        nc.gpsimd.memset(xs.bitcast(I32), 0)
+        nc.vector.memset(w1s_head[:].bitcast(I32), 0)
+        nc.vector.memset(xs_moved[:].bitcast(I32), 0)
+        nc.gpsimd.memset(w1s_rest[:].bitcast(I32), 0)
 
         offs_t = load_list("offs_t", offs)
         xw = [keep.tile([P, T], I32, name=f"xw{s}") for s in range(PASSES)]
@@ -76,35 +72,33 @@ def tile_moe_ser_relu2_kernel(
             nc.sync.dma_start(xw[s][:], x_words[s].rearrange("p t d -> p (t d)").bitcast(I32))
         for q in range(4):
             (nc.scalar if q < 2 else nc.sync).dma_start(xs[32 * q : 32 * q + 4 * PASSES].bitcast(I32), x_scales[:, 4 * q : 4 * q + 4, :].bitcast(I32))
+        ones_raw = keep.tile([P, P], F32)
+        nc.gpsimd.memset(ones_raw[:], 1.0)
         w1_scale_rows = w1_scales.rearrange("e s b i -> (e s) b i")
         w1_rows = w1_words.rearrange("e s p n -> p (e s) n")
         w1 = []
 
         def load_w1(first, last):
-            tile = keep.tile([P, last - first, 2 * H], U8, name=f"w1_{first}", align_bytes=64)
+            if first < 2 * PASSES:
+                tile = keep.tile([P, last - first, 2 * H], U8, name=f"w1_{first}", align_bytes=64)
+            else:
+                place = 4 * late_words + (first - 2 * PASSES) * 2 * H
+                tile = late.tile([P, last - first, 2 * H], U8, name=f"w1_{first}", align_bytes=64, offset=place)
             nc.sync.dma_start(tile[:].bitcast(I32), w1_rows[:, first:last, :].bitcast(I32))
             w1.extend(tile[:, j, :] for j in range(last - first))
 
-        load_w1(0, 6)
-        load_scales(w1s[0], w1_scale_rows[:half])
-        load_w1(6, 12)
-        load_w1(12, 18)
-        load_scales(w1s[1], w1_scale_rows[half:])
-        load_w1(18, 22)
-        load_w1(22, 24)
-        pos1_t = load_list("pos1_t", pos1)
-        pos2_t = load_list("pos2_t", pos2)
-        g1 = keep.tile([P, 2, T], F32)
-        for r in range(2):
-            nc.sync.dma_start(g1[:, r, :], gate1[r])
-        offs2_t = load_list("offs2_t", offs2)
-        w2 = keep.tile([P, E, N], I32, align_bytes=64)
-        nc.sync.dma_start(w2[:], w2_words.rearrange("f s p n d -> p (f s) (n d)").bitcast(I32))
-        load_scales(w2s, w2_scales.rearrange("f s b n -> (f s) b n"))
-        pos3_t = load_list("pos3_t", pos3)
-        pos4_t = load_list("pos4_t", pos4)
-        g2 = keep.tile([P, 2, T], F32)
-        nc.sync.dma_start(g2[:], gate2.rearrange("r p t -> p r t"))
+        load_w1(0, head)
+        load_scales(w1s_head, w1_scale_rows[:head])
+        load_scales(w1s_rest, w1_scale_rows[head:], nc.scalar, (0,))
+        ones = keep.tile([P, P], F32)
+        nc.scalar.activation(ones[:], ones_raw[:], ACT.Relu)
+        load_scales(w1s_rest, w1_scale_rows[head:], nc.scalar, (1,))
+        load_scales(w1s_rest, w1_scale_rows[head:], nc.sync, (2, 3))
+        ident = keep.tile([P, P], F32)
+        nc.gpsimd.affine_select(
+            out=ident[:], in_=ones[:], compare_op=mybir.AluOpType.is_equal, fill=0.0, base=0, pattern=[[-1, P]], channel_multiplier=1
+        )
+        nc.gpsimd.memset(w2s[:].bitcast(I32), 0)
 
         xs_g = keep.tile([P, S], U8, align_bytes=64)
         relu = [keep.tile([P, PACK, P], F32, name=f"relu{e}") for e in range(E)]
@@ -125,11 +119,33 @@ def tile_moe_ser_relu2_kernel(
         xw_early = keep.tile([P, EARLY * C], U32, align_bytes=64)
         for first in range(0, EARLY, 2):
             gather_words(xw_early[:, cols(first, first + 2, C)], 0, first, first + 2)
-        for first, last in BYTE_PIECES:
-            nc.vector.tensor_copy(xs_g[:, cols(first, last, C)], xs[:].indirect(offs_t[:, cols(first, last, C // 16)]))
-        for s in range(1, PASSES):
-            nc.scalar.dma_start(xs_moved[:SHIFTED, s - 1, :].bitcast(I32), xs_g[4 * s : 4 * s + SHIFTED, :].bitcast(I32))
-        xw_late = keep.tile([P, PASSES * S - EARLY * C], U32, tag="shared", align_bytes=64)
+        for pieces, queues in zip(BYTE_GROUPS, ((nc.scalar, nc.scalar), (nc.scalar, nc.scalar))):
+            for first, last in pieces:
+                nc.vector.tensor_copy(xs_g[:, cols(first, last, C)], xs.indirect(offs_t[:, cols(first, last, C // 16)]))
+            slots = cols(pieces[0][0], pieces[-1][1], C)
+            for s in range(1, PASSES):
+                queues[s - 1].dma_start(
+                    xs_moved[:SHIFTED, s - 1, slots].bitcast(I32), xs_g[4 * s : 4 * s + SHIFTED, slots].bitcast(I32)
+                )
+        for e in range(2, 6):
+            load_w1(e * PASSES, (e + 1) * PASSES)
+        load_w1(18, 22)
+        load_w1(22, 24)
+        pos1_t = load_list("pos1_t", pos1)
+        pos2_t = load_list("pos2_t", pos2)
+        g1 = keep.tile([P, 2, T], F32)
+        for r in range(2):
+            nc.sync.dma_start(g1[:, r, :], gate1[r])
+        offs2_t = load_list("offs2_t", offs2)
+        w2 = keep.tile([P, E, N], I32, align_bytes=64)
+        nc.sync.dma_start(w2[:], w2_words.rearrange("f s p n d -> p (f s) (n d)").bitcast(I32))
+        load_scales(w2s, w2_scales.rearrange("f s b n -> (f s) b n"))
+        pos3_t = load_list("pos3_t", pos3)
+        pos4_t = load_list("pos4_t", pos4)
+        g2 = keep.tile([P, 2, T], F32)
+        nc.sync.dma_start(g2[:], gate2.rearrange("r p t -> p r t"))
+
+        xw_late = late.tile([P, late_words], U32, align_bytes=64, offset=0)
 
         def words(s, first, last):
             if s == 0 and first < EARLY:
@@ -147,37 +163,38 @@ def tile_moe_ser_relu2_kernel(
                 lhsT=words(s, e, e + 1).bitcast(FP8X4),
                 lhsT_scale=xs_g[:, cols(e, e + 1, C)] if s == 0 else xs_moved[:, s - 1, cols(e, e + 1, C)],
                 rhs=w1[e * PASSES + s].bitcast(FP4X4),
-                rhs_scale=w1s[e // 4][:, e % 4 * PASSES + s, :],
+                rhs_scale=w1s_head[:, e * PASSES + s, :] if e < FIRST else w1s_rest[:, e * PASSES + s - head, :],
                 start=(s == 0),
                 stop=(s == PASSES - 1),
             )
 
         def rectify(e, acc, planes):
             by_plane = acc[:].rearrange("p (m t) -> p t m", t=PACK)[:, planes, :]
-            if e < E - 1:
-                nc.scalar.activation(relu[e][:, planes, :], by_plane, ACT.Relu)
-            else:
+            if e in (5, 7):
                 nc.vector.tensor_scalar_max(relu[e][:, planes, :], by_plane, 0.0)
+            else:
+                nc.scalar.activation(relu[e][:, planes, :], by_plane, ACT.Relu)
 
-        first_two = [bank_tile(e) for e in range(2)]
+        first_banks = [bank_tile(e) for e in range(FIRST)]
         for s in range(PASSES):
-            for e in range(2):
-                one_pass(first_two[e], e, s)
+            for e in range(FIRST):
+                one_pass(first_banks[e], e, s)
         for e in range(E):
-            if e < 2:
-                acc = first_two[e]
+            if e < FIRST:
+                acc = first_banks[e]
             else:
                 acc = bank_tile(e % 4)
                 for s in range(PASSES):
                     one_pass(acc, e, s)
-            if e < E - 1:
-                rectify(e, acc, slice(0, PACK))
-            else:
+            if e in (3, 6, 7):
                 rectify(e, acc, slice(0, 1))
-                turn(0, 4, 7, 5)
-                turn(0, 7, 8, 6)
+                if e == E - 1:
+                    turn(0, 4, 7, 5)
+                    turn(0, 7, 8, 6)
                 rectify(e, acc, slice(1, PACK))
-            if e == 3:
+            else:
+                rectify(e, acc, slice(0, PACK))
+            if e == 4:
                 turn(0, 0, 4, 4)
         for t in range(1, PACK):
             turn(t, 0, 4, 3)

@@ -22,8 +22,7 @@ MULT = mybir.AluOpType.mult
 ADD = mybir.AluOpType.add
 
 EARLY = 4
-BYTE_GROUPS = (((0, 2),), ((2, 5), (5, 8)))
-FIRST = 2
+BYTE_PIECES = ((0, 3), (3, 6), (6, 8))
 SHIFTED = 112
 C_GROUPS = ((0, 2), (2, 4), (4, 6), (6, 7), (7, 8))
 PAIR_PIECES = ((0, 3), (3, 6), (6, 8))
@@ -47,23 +46,22 @@ def tile_moe_ser_relu2_kernel(
             nc.sync.dma_start(tile[:], dram)
             return tile
 
-        def load_scales(plane, dram, queue=nc.sync, which=range(4)):
+        def load_scales(plane, dram):
             rows = dram.rearrange("g (q r) n -> r q g n", r=4)
-            for r in which:
-                queue.dma_start(plane[r:P:32].bitcast(I32), rows[r].bitcast(I32))
+            for r in range(4):
+                nc.sync.dma_start(plane[r:P:32].bitcast(I32), rows[r].bitcast(I32))
 
-        late = ctx.enter_context(tc.tile_pool(name="late", bufs=1))
-        late_words = PASSES * S - EARLY * C
-        xs_span = late.tile([P, 4 * late_words + (E - 2) * PASSES * 2 * H], U8, align_bytes=64, offset=0)
-        xs = xs_span[:, :T]
+        xs = keep.tile([P, T], U8, tag="shared", align_bytes=64)
         xs_moved = keep.tile([P, PASSES - 1, S], U8, align_bytes=64)
-        head = FIRST * PASSES
+        head = EARLY * PASSES
         w1s_head = keep.tile([P, head, H], U8, align_bytes=64)
         w1s_rest = keep.tile([P, E * PASSES - head, H], U8, align_bytes=64)
         w2s = keep.tile([P, E, N], U8, align_bytes=64)
-        nc.gpsimd.memset(xs.bitcast(I32), 0)
+        nc.gpsimd.memset(xs[:].bitcast(I32), 0)
         nc.vector.memset(w1s_head[:].bitcast(I32), 0)
-        nc.vector.memset(xs_moved[:].bitcast(I32), 0)
+        ones_raw = keep.tile([P, P], F32)
+        nc.vector.memset(ones_raw[:], 1.0)
+        nc.gpsimd.memset(xs_moved[:].bitcast(I32), 0)
         nc.gpsimd.memset(w1s_rest[:].bitcast(I32), 0)
 
         offs_t = load_list("offs_t", offs)
@@ -71,34 +69,30 @@ def tile_moe_ser_relu2_kernel(
         for s in range(PASSES):
             nc.sync.dma_start(xw[s][:], x_words[s].rearrange("p t d -> p (t d)").bitcast(I32))
         for q in range(4):
-            (nc.scalar if q < 2 else nc.sync).dma_start(xs[32 * q : 32 * q + 4 * PASSES].bitcast(I32), x_scales[:, 4 * q : 4 * q + 4, :].bitcast(I32))
-        ones_raw = keep.tile([P, P], F32)
-        nc.gpsimd.memset(ones_raw[:], 1.0)
+            (nc.scalar if q < 2 else nc.sync).dma_start(
+                xs[32 * q : 32 * q + 4 * PASSES].bitcast(I32), x_scales[:, 4 * q : 4 * q + 4, :].bitcast(I32)
+            )
         w1_scale_rows = w1_scales.rearrange("e s b i -> (e s) b i")
         w1_rows = w1_words.rearrange("e s p n -> p (e s) n")
-        w1 = []
+        w1 = [None] * (E * PASSES)
+
+        def load_early_pass(s):
+            tile = keep.tile([P, EARLY, 2 * H], U8, name=f"w1_pass{s}", align_bytes=64)
+            nc.sync.dma_start(tile[:].bitcast(I32), w1_rows[:, s:head:PASSES, :].bitcast(I32))
+            w1[s:head:PASSES] = [tile[:, e, :] for e in range(EARLY)]
 
         def load_w1(first, last):
-            if first < 2 * PASSES:
-                tile = keep.tile([P, last - first, 2 * H], U8, name=f"w1_{first}", align_bytes=64)
-            else:
-                place = 4 * late_words + (first - 2 * PASSES) * 2 * H
-                tile = late.tile([P, last - first, 2 * H], U8, name=f"w1_{first}", align_bytes=64, offset=place)
+            tile = keep.tile([P, last - first, 2 * H], U8, name=f"w1_{first}", align_bytes=64)
             nc.sync.dma_start(tile[:].bitcast(I32), w1_rows[:, first:last, :].bitcast(I32))
-            w1.extend(tile[:, j, :] for j in range(last - first))
+            w1[first:last] = [tile[:, j, :] for j in range(last - first)]
 
-        load_w1(0, head)
-        load_scales(w1s_head, w1_scale_rows[:head])
-        load_scales(w1s_rest, w1_scale_rows[head:], nc.scalar, (0,))
         ones = keep.tile([P, P], F32)
         nc.scalar.activation(ones[:], ones_raw[:], ACT.Relu)
-        load_scales(w1s_rest, w1_scale_rows[head:], nc.scalar, (1,))
-        load_scales(w1s_rest, w1_scale_rows[head:], nc.sync, (2, 3))
-        ident = keep.tile([P, P], F32)
-        nc.gpsimd.affine_select(
-            out=ident[:], in_=ones[:], compare_op=mybir.AluOpType.is_equal, fill=0.0, base=0, pattern=[[-1, P]], channel_multiplier=1
-        )
         nc.gpsimd.memset(w2s[:].bitcast(I32), 0)
+        load_early_pass(0)
+        load_scales(w1s_head, w1_scale_rows[:head])
+        load_early_pass(1)
+        load_early_pass(2)
 
         xs_g = keep.tile([P, S], U8, align_bytes=64)
         relu = [keep.tile([P, PACK, P], F32, name=f"relu{e}") for e in range(E)]
@@ -119,15 +113,12 @@ def tile_moe_ser_relu2_kernel(
         xw_early = keep.tile([P, EARLY * C], U32, align_bytes=64)
         for first in range(0, EARLY, 2):
             gather_words(xw_early[:, cols(first, first + 2, C)], 0, first, first + 2)
-        for pieces, queues in zip(BYTE_GROUPS, ((nc.scalar, nc.scalar), (nc.scalar, nc.scalar))):
-            for first, last in pieces:
-                nc.vector.tensor_copy(xs_g[:, cols(first, last, C)], xs.indirect(offs_t[:, cols(first, last, C // 16)]))
-            slots = cols(pieces[0][0], pieces[-1][1], C)
-            for s in range(1, PASSES):
-                queues[s - 1].dma_start(
-                    xs_moved[:SHIFTED, s - 1, slots].bitcast(I32), xs_g[4 * s : 4 * s + SHIFTED, slots].bitcast(I32)
-                )
-        for e in range(2, 6):
+        for first, last in BYTE_PIECES:
+            nc.vector.tensor_copy(xs_g[:, cols(first, last, C)], xs[:].indirect(offs_t[:, cols(first, last, C // 16)]))
+        for s in range(1, PASSES):
+            nc.sync.dma_start(xs_moved[:SHIFTED, s - 1, :].bitcast(I32), xs_g[4 * s : 4 * s + SHIFTED, :].bitcast(I32))
+        load_scales(w1s_rest, w1_scale_rows[head:])
+        for e in range(EARLY, 6):
             load_w1(e * PASSES, (e + 1) * PASSES)
         load_w1(18, 22)
         load_w1(22, 24)
@@ -145,7 +136,7 @@ def tile_moe_ser_relu2_kernel(
         g2 = keep.tile([P, 2, T], F32)
         nc.sync.dma_start(g2[:], gate2.rearrange("r p t -> p r t"))
 
-        xw_late = late.tile([P, late_words], U32, align_bytes=64, offset=0)
+        xw_late = keep.tile([P, PASSES * S - EARLY * C], U32, tag="shared", align_bytes=64)
 
         def words(s, first, last):
             if s == 0 and first < EARLY:
@@ -163,7 +154,7 @@ def tile_moe_ser_relu2_kernel(
                 lhsT=words(s, e, e + 1).bitcast(FP8X4),
                 lhsT_scale=xs_g[:, cols(e, e + 1, C)] if s == 0 else xs_moved[:, s - 1, cols(e, e + 1, C)],
                 rhs=w1[e * PASSES + s].bitcast(FP4X4),
-                rhs_scale=w1s_head[:, e * PASSES + s, :] if e < FIRST else w1s_rest[:, e * PASSES + s - head, :],
+                rhs_scale=w1s_head[:, e * PASSES + s, :] if e < EARLY else w1s_rest[:, e * PASSES + s - head, :],
                 start=(s == 0),
                 stop=(s == PASSES - 1),
             )
@@ -175,30 +166,35 @@ def tile_moe_ser_relu2_kernel(
             else:
                 nc.scalar.activation(relu[e][:, planes, :], by_plane, ACT.Relu)
 
-        first_banks = [bank_tile(e) for e in range(FIRST)]
-        for s in range(PASSES):
-            for e in range(FIRST):
-                one_pass(first_banks[e], e, s)
-        for e in range(E):
-            if e < FIRST:
-                acc = first_banks[e]
+        early_banks = [bank_tile(e) for e in range(EARLY)]
+        for e in range(EARLY):
+            one_pass(early_banks[e], e, 0)
+        for e in range(EARLY):
+            for s in range(1, PASSES):
+                one_pass(early_banks[e], e, s)
+            rectify(e, early_banks[e], slice(0, PACK))
+        for e in range(EARLY, E):
+            acc = bank_tile((5, 6, 7, 0)[e - EARLY])
+            for s in range(PASSES):
+                one_pass(acc, e, s)
+            if e == EARLY:
+                ident = keep.tile([P, P], F32, name=f"w1_{head}", align_bytes=64)
+                nc.gpsimd.affine_select(
+                    out=ident[:], in_=ones[:], compare_op=mybir.AluOpType.is_equal, fill=0.0, base=0, pattern=[[-1, P]], channel_multiplier=1
+                )
+            if e == 5:
+                turn(0, 0, EARLY, 4)
+            if e < 6:
+                rectify(e, acc, slice(0, PACK))
             else:
-                acc = bank_tile(e % 4)
-                for s in range(PASSES):
-                    one_pass(acc, e, s)
-            if e in (3, 6, 7):
                 rectify(e, acc, slice(0, 1))
                 if e == E - 1:
-                    turn(0, 4, 7, 5)
-                    turn(0, 7, 8, 6)
+                    turn(0, 4, 7, 1)
+                    turn(0, 7, 8, 2)
                 rectify(e, acc, slice(1, PACK))
-            else:
-                rectify(e, acc, slice(0, PACK))
-            if e == 4:
-                turn(0, 0, 4, 4)
         for t in range(1, PACK):
-            turn(t, 0, 4, 3)
-            turn(t, 4, 8, 6)
+            turn(t, 0, 4, 1)
+            turn(t, 4, 8, 2)
 
         c_plane = [keep.tile([P, T], BF16, name=f"c{t}") for t in range(2)]
         c_pair = keep.tile([P, T, 2], BF16)

@@ -205,18 +205,32 @@ def tile_moe_ser_relu2_kernel(
         def gated(dst, window, offsets, gate):
             nc.vector.tensor_tensor(dst, window[:].indirect(offsets), gate, MULT)
 
+        ident_bf = keep.tile([P, P], BF16)
+        nc.scalar.copy(ident_bf[:], ident[:])
         for t in range(2):
             ga = keep.tile([P, T], F32, name=f"ga{t}")
             gb = keep.tile([P, T], F32, name=f"gb{t}")
             gated(ga[:], h[t], pos1_t[:], g1[:, 0, :])
             gated(gb[:], h[t], pos2_t[:], g1[:, 1, :])
-            nc.vector.tensor_tensor(c_plane[t][:], ga[:], gb[:], ADD)
-            for e in range(E):
+            sums = bank_tile(3 + t)
+            for b in range(T // P):
+                block = cols(b, b + 1, P)
+                nc.tensor.matmul(sums[:, block], ga[:, block], ident[:], start=True, stop=False, is_transpose=True)
+                nc.tensor.matmul(sums[:, block], gb[:, block], ident[:], start=False, stop=True, is_transpose=True)
+            turned = keep.tile([P, T], BF16, name=f"turned{t}")
+            nc.scalar.copy(turned[:], sums[:])
+            back = psum.tile([P, T], BF16, name=f"bank{5 + t}")
+            for b in range(T // P):
+                block = cols(b, b + 1, P)
+                nc.tensor.transpose(back[:, block], turned[:, block], ident_bf[:])
+            nc.scalar.copy(c_plane[t][:], back[:])
+        for t in range(2):
+            for first, last in PAIR_PIECES:
                 nc.scalar.activation(
-                    low_pairs[:, cols(e, e + 1, C), t], c_plane[t][:].indirect(offs2_t[:, cols(e, e + 1, C // 16)]), ACT.Copy
+                    low_pairs[:, cols(first, last, C), t], c_plane[t][:].indirect(offs2_t[:, cols(first, last, C // 16)]), ACT.Copy
                 )
-        ga_pair = keep.tile([P, 2, T], F32, tag="ga0")
-        gb_pair = keep.tile([P, 2, T], F32, tag="gb0")
+        ga_pair = keep.tile([P, 2, T], F32)
+        gb_pair = keep.tile([P, 2, T], F32)
         for j in range(2):
             gated(ga_pair[:, j, :], h[2 + j], pos1_t[:], g1[:, 0, :])
             gated(gb_pair[:, j, :], h[2 + j], pos2_t[:], g1[:, 1, :])
@@ -252,12 +266,15 @@ def tile_moe_ser_relu2_kernel(
 
         for first, last in PAIR_PIECES:
             gather_pairs(first, last)
-        for j, (first, last) in enumerate(C_GROUPS):
-            slots = cols(first, last, C)
-            nc.vector.tensor_copy(cq[:, slots], slot_pairs[:, :, slots].rearrange("p j n -> p n j"))
-            if j > 0:
-                second_layer(*C_GROUPS[j - 1])
-        second_layer(*C_GROUPS[-1])
+        for first in range(0, E, 2):
+            slots = cols(first, first + 2, C)
+            pairs = slot_pairs[:, :, slots].rearrange("p j n -> p n j")
+            if first >= E // 2:
+                nc.scalar.copy(cq[:, slots].bitcast(U32), pairs.bitcast(U32))
+            else:
+                nc.vector.tensor_copy(cq[:, slots], pairs)
+        for group in C_GROUPS:
+            second_layer(*group)
 
         ya = keep.tile([P, T], F32)
         yb = keep.tile([P, T], F32)

@@ -90,7 +90,8 @@ def tile_moe_ser_relu2_kernel(
         nc.scalar.activation(ones[:], ones_raw[:], ACT.Relu)
         nc.gpsimd.memset(w2s[:].bitcast(I32), 0)
         load_early_pass(0)
-        load_scales(w1s_head, w1_scale_rows[:head])
+        for j in range(2):
+            load_scales(w1s_head[:, cols(j, j + 1, head // 2)], w1_scale_rows[cols(j, j + 1, head // 2)])
         load_early_pass(1)
         load_early_pass(2)
 
@@ -117,7 +118,8 @@ def tile_moe_ser_relu2_kernel(
             nc.vector.tensor_copy(xs_g[:, cols(first, last, C)], xs[:].indirect(offs_t[:, cols(first, last, C // 16)]))
         for s in range(1, PASSES):
             nc.sync.dma_start(xs_moved[:SHIFTED, s - 1, :].bitcast(I32), xs_g[4 * s : 4 * s + SHIFTED, :].bitcast(I32))
-        load_scales(w1s_rest, w1_scale_rows[head:])
+        for j in range(2):
+            load_scales(w1s_rest[:, cols(j, j + 1, head // 2)], w1_scale_rows[cols(2 + j, 3 + j, head // 2)])
         for e in range(EARLY, 6):
             load_w1(e * PASSES, (e + 1) * PASSES)
         load_w1(18, 22)

@@ -23,7 +23,7 @@ ADD = mybir.AluOpType.add
 
 EARLY = 4
 BYTE_PIECES = ((0, 3), (3, 6), (6, 8))
-SHIFTED = 112
+SHIFTED = 100
 C_GROUPS = ((0, 2), (2, 4), (4, 6), (6, 7), (7, 8))
 PAIR_PIECES = ((0, 3), (3, 6), (6, 8))
 OUT_PIECES = ((0, 3), (3, 4))
@@ -123,7 +123,8 @@ def tile_moe_ser_relu2_kernel(
         for e in range(EARLY, 6):
             load_w1(e * PASSES, (e + 1) * PASSES)
         load_w1(18, 22)
-        load_w1(22, 24)
+        load_w1(22, 23)
+        load_w1(23, 24)
         pos1_t = load_list("pos1_t", pos1)
         pos2_t = load_list("pos2_t", pos2)
         g1 = keep.tile([P, 2, T], F32)
@@ -233,10 +234,16 @@ def tile_moe_ser_relu2_kernel(
                 )
         ga_pair = keep.tile([P, 2, T], F32)
         gb_pair = keep.tile([P, 2, T], F32)
-        for j in range(2):
-            gated(ga_pair[:, j, :], h[2 + j], pos1_t[:], g1[:, 0, :])
-            gated(gb_pair[:, j, :], h[2 + j], pos2_t[:], g1[:, 1, :])
-        nc.vector.tensor_tensor(c_pair[:], ga_pair[:].rearrange("p t n -> p n t"), gb_pair[:].rearrange("p t n -> p n t"), ADD)
+        gated(ga_pair[:, 0, :], h[2], pos1_t[:], g1[:, 0, :])
+        gated(gb_pair[:, 0, :], h[2], pos2_t[:], g1[:, 1, :])
+        gated(ga_pair[:, 1, :], h[3], pos1_t[:], g1[:, 0, :])
+        halves = [cols(j, j + 1, T // 2) for j in range(2)]
+        for j, tokens in enumerate(halves):
+            gated(gb_pair[:, 1, tokens], h[3], pos2_t[:, cols(j, j + 1, T // 32)], g1[:, 1, tokens])
+        for tokens in halves:
+            nc.vector.tensor_tensor(
+                c_pair[:, tokens], ga_pair[:, :, tokens].rearrange("p t n -> p n t"), gb_pair[:, :, tokens].rearrange("p t n -> p n t"), ADD
+            )
 
         codes = keep.tile([P, S], U32, align_bytes=64)
         scales = keep.tile([P, S], U8, align_bytes=64)

@@ -23,7 +23,6 @@ ADD = mybir.AluOpType.add
 
 EARLY = 4
 BYTE_PIECES = ((0, 3), (3, 6), (6, 8))
-SHIFTED = 100
 C_GROUPS = ((0, 2), (2, 4), (4, 6), (6, 7), (7, 8))
 PAIR_PIECES = ((0, 3), (3, 6), (6, 8))
 OUT_PIECES = ((0, 3), (3, 4))
@@ -51,14 +50,16 @@ def tile_moe_ser_relu2_kernel(
             for r in range(4):
                 nc.sync.dma_start(plane[r:P:32].bitcast(I32), rows[r].bitcast(I32))
 
-        xs = keep.tile([P, T], U8, tag="shared", align_bytes=64)
-        xs_moved = keep.tile([P, PASSES - 1, S], U8, align_bytes=64)
+        xs_a = keep.tile([P, T], U8, tag="shared_a", align_bytes=64)
+        xs_b = keep.tile([P, T], U8, tag="shared_b", align_bytes=64)
+        xs_moved = keep.tile([P, S], U8, align_bytes=64)
         head = EARLY * PASSES
         w1s_head = keep.tile([P, head, H], U8, align_bytes=64)
         w1s_rest = keep.tile([P, E * PASSES - head, H], U8, align_bytes=64)
         w2s = keep.tile([P, E, N], U8, align_bytes=64)
-        nc.gpsimd.memset(xs[:].bitcast(I32), 0)
+        nc.gpsimd.memset(xs_a[:].bitcast(I32), 0)
         nc.vector.memset(w1s_head[:].bitcast(I32), 0)
+        nc.vector.memset(xs_b[:].bitcast(I32), 0)
         ones_raw = keep.tile([P, P], F32)
         nc.vector.memset(ones_raw[:], 1.0)
         nc.gpsimd.memset(xs_moved[:].bitcast(I32), 0)
@@ -69,17 +70,10 @@ def tile_moe_ser_relu2_kernel(
         for s in range(PASSES):
             nc.sync.dma_start(xw[s][:], x_words[s].rearrange("p t d -> p (t d)").bitcast(I32))
         for q in range(4):
-            (nc.scalar if q < 2 else nc.sync).dma_start(
-                xs[32 * q : 32 * q + 4 * PASSES].bitcast(I32), x_scales[:, 4 * q : 4 * q + 4, :].bitcast(I32)
-            )
+            nc.scalar.dma_start(xs_a[32 * q : 32 * q + 8].bitcast(I32), x_scales[0:PASSES:2, 4 * q : 4 * q + 4, :].bitcast(I32))
         w1_scale_rows = w1_scales.rearrange("e s b i -> (e s) b i")
         w1_rows = w1_words.rearrange("e s p n -> p (e s) n")
         w1 = [None] * (E * PASSES)
-
-        def load_early_pass(s):
-            tile = keep.tile([P, EARLY, 2 * H], U8, name=f"w1_pass{s}", align_bytes=64)
-            nc.sync.dma_start(tile[:].bitcast(I32), w1_rows[:, s:head:PASSES, :].bitcast(I32))
-            w1[s:head:PASSES] = [tile[:, e, :] for e in range(EARLY)]
 
         def load_w1(first, last):
             tile = keep.tile([P, last - first, 2 * H], U8, name=f"w1_{first}", align_bytes=64)
@@ -89,13 +83,15 @@ def tile_moe_ser_relu2_kernel(
         ones = keep.tile([P, P], F32)
         nc.scalar.activation(ones[:], ones_raw[:], ACT.Relu)
         nc.gpsimd.memset(w2s[:].bitcast(I32), 0)
-        load_early_pass(0)
-        for j in range(2):
-            load_scales(w1s_head[:, cols(j, j + 1, head // 2)], w1_scale_rows[cols(j, j + 1, head // 2)])
-        load_early_pass(1)
-        load_early_pass(2)
+        load_scales(w1s_head, w1_scale_rows[:head])
+        pass1_rows = x_scales[1].rearrange("(q r) n -> r q n", r=4)
+        for r in range(4):
+            nc.sync.dma_start(xs_b[r:P:32].bitcast(I32), pass1_rows[r].bitcast(I32))
+        for e in range(EARLY):
+            load_w1(e * PASSES, (e + 1) * PASSES)
 
         xs_g = keep.tile([P, S], U8, align_bytes=64)
+        xs_gb = keep.tile([P, S], U8, align_bytes=64)
         relu = [keep.tile([P, PACK, P], F32, name=f"relu{e}") for e in range(E)]
         h = [keep.tile([P, S], F32, name=f"h{t}") for t in range(PACK)]
 
@@ -111,15 +107,16 @@ def tile_moe_ser_relu2_kernel(
                 nc.tensor.transpose(bank[:, cols(e - first, e - first + 1, C)], relu[e][:, t, :], ident[:])
             nc.scalar.activation(h[t][:, cols(first, last, C)], bank[:, cols(0, last - first, C)], ACT.Square)
 
-        xw_early = keep.tile([P, EARLY * C], U32, align_bytes=64)
-        for first in range(0, EARLY, 2):
-            gather_words(xw_early[:, cols(first, first + 2, C)], 0, first, first + 2)
+        xw_first = keep.tile([P, 2 * C], U32, align_bytes=64)
+        gather_words(xw_first[:], 0, 0, 2)
         for first, last in BYTE_PIECES:
-            nc.vector.tensor_copy(xs_g[:, cols(first, last, C)], xs[:].indirect(offs_t[:, cols(first, last, C // 16)]))
-        for s in range(1, PASSES):
-            nc.sync.dma_start(xs_moved[:SHIFTED, s - 1, :].bitcast(I32), xs_g[4 * s : 4 * s + SHIFTED, :].bitcast(I32))
-        for j in range(2):
-            load_scales(w1s_rest[:, cols(j, j + 1, head // 2)], w1_scale_rows[cols(2 + j, 3 + j, head // 2)])
+            nc.vector.tensor_copy(xs_g[:, cols(first, last, C)], xs_a[:].indirect(offs_t[:, cols(first, last, C // 16)]))
+        rest_rows = w1_scale_rows[head:].rearrange("g (q r) n -> r q g n", r=4)
+        for r in range(4):
+            nc.sync.dma_start(w1s_rest[r:P:32].bitcast(I32), rest_rows[r].bitcast(I32))
+            if r == 0:
+                for m in range(4):
+                    nc.sync.dma_start(xs_moved[m:P:32].bitcast(I32), xs_g[4 + m : P : 32].bitcast(I32))
         for e in range(EARLY, 6):
             load_w1(e * PASSES, (e + 1) * PASSES)
         load_w1(18, 22)
@@ -139,23 +136,29 @@ def tile_moe_ser_relu2_kernel(
         g2 = keep.tile([P, 2, T], F32)
         nc.sync.dma_start(g2[:], gate2.rearrange("r p t -> p r t"))
 
-        xw_late = keep.tile([P, PASSES * S - EARLY * C], U32, tag="shared", align_bytes=64)
+        xw_next = keep.tile([P, (PASSES - 1) * 2 * C], U32, tag="shared_a", align_bytes=64)
+        for s in range(1, PASSES):
+            gather_words(xw_next[:, cols(2 * s - 2, 2 * s, C)], s, 0, 2)
+        for first, last in BYTE_PIECES:
+            nc.vector.tensor_copy(xs_gb[:, cols(first, last, C)], xs_b[:].indirect(offs_t[:, cols(first, last, C // 16)]))
+        xw_late = keep.tile([P, PASSES * (E - 2) * C], U32, tag="shared_b", align_bytes=64)
 
         def words(s, first, last):
-            if s == 0 and first < EARLY:
-                return xw_early[:, cols(first, last, C)]
-            return xw_late[:, cols(s * E - EARLY + first, s * E - EARLY + last, C)]
+            if first >= 2:
+                return xw_late[:, cols(s * (E - 2) - 2 + first, s * (E - 2) - 2 + last, C)]
+            if s == 0:
+                return xw_first[:, cols(first, last, C)]
+            return xw_next[:, cols(2 * s - 2 + first, 2 * s - 2 + last, C)]
 
-        for first in range(0, E, 2):
+        for first, last in ((2, 4), (4, 6), (6, 7), (7, 8)):
             for s in range(PASSES):
-                if s > 0 or first >= EARLY:
-                    gather_words(words(s, first, first + 2), s, first, first + 2)
+                gather_words(words(s, first, last), s, first, last)
 
         def one_pass(acc, e, s):
             nc.tensor.matmul_mx(
                 out=acc[:],
                 lhsT=words(s, e, e + 1).bitcast(FP8X4),
-                lhsT_scale=xs_g[:, cols(e, e + 1, C)] if s == 0 else xs_moved[:, s - 1, cols(e, e + 1, C)],
+                lhsT_scale=(xs_g, xs_gb, xs_moved)[s][:, cols(e, e + 1, C)],
                 rhs=w1[e * PASSES + s].bitcast(FP4X4),
                 rhs_scale=w1s_head[:, e * PASSES + s, :] if e < EARLY else w1s_rest[:, e * PASSES + s - head, :],
                 start=(s == 0),
@@ -164,37 +167,37 @@ def tile_moe_ser_relu2_kernel(
 
         def rectify(e, acc, planes):
             by_plane = acc[:].rearrange("p (m t) -> p t m", t=PACK)[:, planes, :]
-            if e in (5, 7):
+            if e == 7:
                 nc.vector.tensor_scalar_max(relu[e][:, planes, :], by_plane, 0.0)
             else:
                 nc.scalar.activation(relu[e][:, planes, :], by_plane, ACT.Relu)
 
-        early_banks = [bank_tile(e) for e in range(EARLY)]
+        banks = [bank_tile(b) for b in (0, 1, 2, 3, 5, 6, 7)]
+        for first in range(0, EARLY, 2):
+            for s in range(PASSES - 1):
+                for e in range(first, first + 2):
+                    one_pass(banks[e], e, s)
         for e in range(EARLY):
-            one_pass(early_banks[e], e, 0)
-        for e in range(EARLY):
-            for s in range(1, PASSES):
-                one_pass(early_banks[e], e, s)
-            rectify(e, early_banks[e], slice(0, PACK))
-        for e in range(EARLY, E):
-            acc = bank_tile((5, 6, 7, 0)[e - EARLY])
+            one_pass(banks[e], e, PASSES - 1)
+            rectify(e, banks[e], slice(0, PACK))
+        for e in range(EARLY, 6):
+            for s in range(PASSES):
+                one_pass(banks[e], e, s)
+            rectify(e, banks[e], slice(0, PACK))
+        ident = keep.tile([P, P], F32, name=f"w1_{head}", align_bytes=64)
+        nc.gpsimd.affine_select(
+            out=ident[:], in_=ones[:], compare_op=mybir.AluOpType.is_equal, fill=0.0, base=0, pattern=[[-1, P]], channel_multiplier=1
+        )
+        turn(0, 0, EARLY, 4)
+        for e in range(6, E):
+            acc = banks[e] if e == 6 else bank_tile(0)
             for s in range(PASSES):
                 one_pass(acc, e, s)
-            if e == EARLY:
-                ident = keep.tile([P, P], F32, name=f"w1_{head}", align_bytes=64)
-                nc.gpsimd.affine_select(
-                    out=ident[:], in_=ones[:], compare_op=mybir.AluOpType.is_equal, fill=0.0, base=0, pattern=[[-1, P]], channel_multiplier=1
-                )
-            if e == 5:
-                turn(0, 0, EARLY, 4)
-            if e < 6:
-                rectify(e, acc, slice(0, PACK))
-            else:
-                rectify(e, acc, slice(0, 1))
-                if e == E - 1:
-                    turn(0, 4, 7, 1)
-                    turn(0, 7, 8, 2)
-                rectify(e, acc, slice(1, PACK))
+            rectify(e, acc, slice(0, 1))
+            if e == E - 1:
+                turn(0, 4, 7, 1)
+                turn(0, 7, 8, 2)
+            rectify(e, acc, slice(1, PACK))
         for t in range(1, PACK):
             turn(t, 0, 4, 1)
             turn(t, 4, 8, 2)

@@ -297,11 +297,13 @@ def tile_moe_ser_relu2_kernel(
             nc.vector.tensor_tensor(res[:, tokens], ya[:, tokens], yb[:, tokens], ADD)
             nc.sync.dma_start(out[:, tokens], res[:, tokens])
 
-        for j, (first, last) in enumerate(OUT_PIECES):
+        fetched = keep.tile([P, T], F32)
+        for first, last in OUT_PIECES:
             tokens = cols(first, last, P)
-            entries = cols(first, last, P // 16)
-            gated(ya[:, tokens], y, pos3_t[:, entries], g2[:, 0, tokens])
-            if j > 0:
-                finish(*OUT_PIECES[j - 1])
-            gated(yb[:, tokens], y, pos4_t[:, entries], g2[:, 1, tokens])
-        finish(*OUT_PIECES[-1])
+            nc.scalar.activation(fetched[:, tokens], y[:].indirect(pos4_t[:, cols(first, last, P // 16)]), ACT.Copy)
+            gated(ya[:, tokens], y, pos3_t[:, cols(first, last, P // 16)], g2[:, 0, tokens])
+        for first, last in OUT_PIECES:
+            tokens = cols(first, last, P)
+            nc.vector.tensor_tensor(yb[:, tokens], fetched[:, tokens], g2[:, 1, tokens], MULT)
+        for piece in OUT_PIECES:
+            finish(*piece)

@@ -90,6 +90,9 @@ def tile_moe_ser_relu2_kernel(
         for e in range(EARLY):
             load_w1(e * PASSES, (e + 1) * PASSES)
 
+        def entries(tile, first, last, width):
+            return tile[:, cols(first, last, width // 16)]
+
         xs_g = keep.tile([P, S], U8, align_bytes=64)
         xs_gb = keep.tile([P, S], U8, align_bytes=64)
         relu = [keep.tile([P, PACK, P], F32, name=f"relu{e}") for e in range(E)]
@@ -211,9 +214,7 @@ def tile_moe_ser_relu2_kernel(
         def gated(dst, window, offsets, gate):
             nc.vector.tensor_tensor(dst, window[:].indirect(offsets), gate, MULT)
 
-        ident_bf = keep.tile([P, P], BF16)
-        nc.scalar.copy(ident_bf[:], ident[:])
-        for t in range(2):
+        def add_turned(t):
             ga = keep.tile([P, T], F32, name=f"ga{t}")
             gb = keep.tile([P, T], F32, name=f"gb{t}")
             gated(ga[:], h[t], pos1_t[:], g1[:, 0, :])
@@ -223,26 +224,42 @@ def tile_moe_ser_relu2_kernel(
                 block = cols(b, b + 1, P)
                 nc.tensor.matmul(sums[:, block], ga[:, block], ident[:], start=True, stop=False, is_transpose=True)
                 nc.tensor.matmul(sums[:, block], gb[:, block], ident[:], start=False, stop=True, is_transpose=True)
-            turned = keep.tile([P, T], BF16, name=f"turned{t}")
+            return sums
+
+        def turn_back(t, sums):
+            turned = keep.tile([P, T], BF16, name="turned")
             nc.scalar.copy(turned[:], sums[:])
             back = psum.tile([P, T], BF16, name=f"bank{5 + t}")
             for b in range(T // P):
                 block = cols(b, b + 1, P)
                 nc.tensor.transpose(back[:, block], turned[:, block], ident_bf[:])
-            nc.scalar.copy(c_plane[t][:], back[:])
-        for t in range(2):
-            for first, last in PAIR_PIECES:
-                nc.scalar.activation(
-                    low_pairs[:, cols(first, last, C), t], c_plane[t][:].indirect(offs2_t[:, cols(first, last, C // 16)]), ACT.Copy
-                )
+            return back
+
+        def gather_plane(t, first, last):
+            nc.scalar.activation(low_pairs[:, cols(first, last, C), t], c_plane[t][:].indirect(entries(offs2_t, first, last, C)), ACT.Copy)
+
+        ident_bf = keep.tile([P, P], BF16)
+        nc.scalar.copy(ident_bf[:], ident[:])
+        sums = [add_turned(t) for t in range(2)]
+        back = turn_back(0, sums[0])
+        second_last = keep.tile([P, T], F32)
+        nc.scalar.activation(second_last[:], h[3][:].indirect(pos2_t[:]), ACT.Copy)
+        nc.scalar.copy(c_plane[0][:], back[:])
+        gather_plane(0, *PAIR_PIECES[0])
+        back = turn_back(1, sums[1])
+        gather_plane(0, *PAIR_PIECES[1])
+        nc.scalar.copy(c_plane[1][:], back[:])
+        gather_plane(0, *PAIR_PIECES[2])
+        for piece in PAIR_PIECES:
+            gather_plane(1, *piece)
         ga_pair = keep.tile([P, 2, T], F32)
         gb_pair = keep.tile([P, 2, T], F32)
         gated(ga_pair[:, 0, :], h[2], pos1_t[:], g1[:, 0, :])
         gated(gb_pair[:, 0, :], h[2], pos2_t[:], g1[:, 1, :])
         gated(ga_pair[:, 1, :], h[3], pos1_t[:], g1[:, 0, :])
         halves = [cols(j, j + 1, T // 2) for j in range(2)]
-        for j, tokens in enumerate(halves):
-            gated(gb_pair[:, 1, tokens], h[3], pos2_t[:, cols(j, j + 1, T // 32)], g1[:, 1, tokens])
+        for tokens in halves:
+            nc.vector.tensor_tensor(gb_pair[:, 1, tokens], second_last[:, tokens], g1[:, 1, tokens], MULT)
         for tokens in halves:
             nc.vector.tensor_tensor(
                 c_pair[:, tokens], ga_pair[:, :, tokens].rearrange("p t n -> p n t"), gb_pair[:, :, tokens].rearrange("p t n -> p n t"), ADD

@@ -62,7 +62,7 @@ def tile_moe_ser_relu2_kernel(
         nc.vector.memset(xs_b[:].bitcast(I32), 0)
         ones_raw = keep.tile([P, P], F32)
         nc.vector.memset(ones_raw[:], 1.0)
-        nc.gpsimd.memset(xs_moved[:].bitcast(I32), 0)
+        nc.vector.memset(xs_moved[:].bitcast(I32), 0)
         nc.gpsimd.memset(w1s_rest[:].bitcast(I32), 0)
 
         offs_t = load_list("offs_t", offs)
@@ -82,7 +82,7 @@ def tile_moe_ser_relu2_kernel(
 
         ones = keep.tile([P, P], F32)
         nc.scalar.activation(ones[:], ones_raw[:], ACT.Relu)
-        nc.gpsimd.memset(w2s[:].bitcast(I32), 0)
+        nc.vector.memset(w2s[:].bitcast(I32), 0)
         load_scales(w1s_head, w1_scale_rows[:head])
         pass1_rows = x_scales[1].rearrange("(q r) n -> r q n", r=4)
         for r in range(4):
@@ -115,11 +115,10 @@ def tile_moe_ser_relu2_kernel(
         for first, last in BYTE_PIECES:
             nc.vector.tensor_copy(xs_g[:, cols(first, last, C)], xs_a[:].indirect(offs_t[:, cols(first, last, C // 16)]))
         rest_rows = w1_scale_rows[head:].rearrange("g (q r) n -> r q g n", r=4)
+        for m in range(4):
+            nc.sync.dma_start(xs_moved[m:P:32].bitcast(I32), xs_g[4 + m : P : 32].bitcast(I32))
         for r in range(4):
             nc.sync.dma_start(w1s_rest[r:P:32].bitcast(I32), rest_rows[r].bitcast(I32))
-            if r == 0:
-                for m in range(4):
-                    nc.sync.dma_start(xs_moved[m:P:32].bitcast(I32), xs_g[4 + m : P : 32].bitcast(I32))
         for e in range(EARLY, 6):
             load_w1(e * PASSES, (e + 1) * PASSES)
         load_w1(18, 22)

@@ -22,6 +22,7 @@ MULT = mybir.AluOpType.mult
 ADD = mybir.AluOpType.add
 
 EARLY = 4
+OWN = 192
 BYTE_PIECES = ((0, 3), (3, 6), (6, 8))
 C_GROUPS = ((0, 2), (2, 4), (4, 6), (6, 7), (7, 8))
 PAIR_PIECES = ((0, 3), (3, 6), (6, 8))
@@ -241,8 +242,8 @@ def tile_moe_ser_relu2_kernel(
         nc.scalar.copy(ident_bf[:], ident[:])
         sums = [add_turned(t) for t in range(2)]
         back = turn_back(0, sums[0])
-        second_last = keep.tile([P, T], F32)
-        nc.scalar.activation(second_last[:], h[3][:].indirect(pos2_t[:]), ACT.Copy)
+        second_last = keep.tile([P, T - OWN], F32)
+        nc.scalar.activation(second_last[:], h[3][:].indirect(pos2_t[:, OWN // 16 :]), ACT.Copy)
         nc.scalar.copy(c_plane[0][:], back[:])
         gather_plane(0, *PAIR_PIECES[0])
         back = turn_back(1, sums[1])
@@ -256,9 +257,9 @@ def tile_moe_ser_relu2_kernel(
         gated(ga_pair[:, 0, :], h[2], pos1_t[:], g1[:, 0, :])
         gated(gb_pair[:, 0, :], h[2], pos2_t[:], g1[:, 1, :])
         gated(ga_pair[:, 1, :], h[3], pos1_t[:], g1[:, 0, :])
-        halves = [cols(j, j + 1, T // 2) for j in range(2)]
-        for tokens in halves:
-            nc.vector.tensor_tensor(gb_pair[:, 1, tokens], second_last[:, tokens], g1[:, 1, tokens], MULT)
+        halves = [slice(0, OWN), slice(OWN, T)]
+        gated(gb_pair[:, 1, halves[0]], h[3], pos2_t[:, : OWN // 16], g1[:, 1, halves[0]])
+        nc.vector.tensor_tensor(gb_pair[:, 1, halves[1]], second_last[:], g1[:, 1, halves[1]], MULT)
         for tokens in halves:
             nc.vector.tensor_tensor(
                 c_pair[:, tokens], ga_pair[:, :, tokens].rearrange("p t n -> p n t"), gb_pair[:, :, tokens].rearrange("p t n -> p n t"), ADD

@@ -22,7 +22,6 @@ MULT = mybir.AluOpType.mult
 ADD = mybir.AluOpType.add
 
 EARLY = 4
-OWN = 192
 BYTE_PIECES = ((0, 3), (3, 6), (6, 8))
 C_GROUPS = ((0, 2), (2, 4), (4, 6), (6, 7), (7, 8))
 PAIR_PIECES = ((0, 3), (3, 6), (6, 8))
@@ -201,9 +200,8 @@ def tile_moe_ser_relu2_kernel(
                 turn(0, 4, 7, 1)
                 turn(0, 7, 8, 2)
             rectify(e, acc, slice(1, PACK))
-        for t in range(1, PACK):
-            turn(t, 0, 4, 1)
-            turn(t, 4, 8, 2)
+        for j in range(2, 2 * PACK - 1):
+            turn(j // 2, 4 * (j % 2), 4 * (j % 2) + 4, (j - 1) % 3)
 
         c_plane = [keep.tile([P, T], BF16, name=f"c{t}") for t in range(2)]
         c_pair = keep.tile([P, T, 2], BF16)
@@ -219,16 +217,19 @@ def tile_moe_ser_relu2_kernel(
             gb = keep.tile([P, T], F32, name=f"gb{t}")
             gated(ga[:], h[t], pos1_t[:], g1[:, 0, :])
             gated(gb[:], h[t], pos2_t[:], g1[:, 1, :])
-            sums = bank_tile(3 + t)
+            sums = bank_tile(1)
             for b in range(T // P):
                 block = cols(b, b + 1, P)
                 nc.tensor.matmul(sums[:, block], ga[:, block], ident[:], start=True, stop=False, is_transpose=True)
                 nc.tensor.matmul(sums[:, block], gb[:, block], ident[:], start=False, stop=True, is_transpose=True)
             return sums
 
-        def turn_back(t, sums):
+        def round_sums(sums):
             turned = keep.tile([P, T], BF16, name="turned")
             nc.scalar.copy(turned[:], sums[:])
+            return turned
+
+        def turn_back(t, turned):
             back = psum.tile([P, T], BF16, name=f"bank{5 + t}")
             for b in range(T // P):
                 block = cols(b, b + 1, P)
@@ -240,13 +241,15 @@ def tile_moe_ser_relu2_kernel(
 
         ident_bf = keep.tile([P, P], BF16)
         nc.scalar.copy(ident_bf[:], ident[:])
-        sums = [add_turned(t) for t in range(2)]
-        back = turn_back(0, sums[0])
-        second_last = keep.tile([P, T - OWN], F32)
-        nc.scalar.activation(second_last[:], h[3][:].indirect(pos2_t[:, OWN // 16 :]), ACT.Copy)
+        second_last = keep.tile([P, T], F32)
+        nc.scalar.activation(second_last[:], h[2][:].indirect(pos2_t[:]), ACT.Copy)
+        turned = round_sums(add_turned(0))
+        turn(3, 4, 8, 2)
+        back = turn_back(0, turned)
+        sums = add_turned(1)
         nc.scalar.copy(c_plane[0][:], back[:])
         gather_plane(0, *PAIR_PIECES[0])
-        back = turn_back(1, sums[1])
+        back = turn_back(1, round_sums(sums))
         gather_plane(0, *PAIR_PIECES[1])
         nc.scalar.copy(c_plane[1][:], back[:])
         gather_plane(0, *PAIR_PIECES[2])
@@ -255,11 +258,11 @@ def tile_moe_ser_relu2_kernel(
         ga_pair = keep.tile([P, 2, T], F32)
         gb_pair = keep.tile([P, 2, T], F32)
         gated(ga_pair[:, 0, :], h[2], pos1_t[:], g1[:, 0, :])
-        gated(gb_pair[:, 0, :], h[2], pos2_t[:], g1[:, 1, :])
+        nc.vector.tensor_tensor(gb_pair[:, 0, :], second_last[:], g1[:, 1, :], MULT)
         gated(ga_pair[:, 1, :], h[3], pos1_t[:], g1[:, 0, :])
-        halves = [slice(0, OWN), slice(OWN, T)]
-        gated(gb_pair[:, 1, halves[0]], h[3], pos2_t[:, : OWN // 16], g1[:, 1, halves[0]])
-        nc.vector.tensor_tensor(gb_pair[:, 1, halves[1]], second_last[:], g1[:, 1, halves[1]], MULT)
+        halves = [cols(j, j + 1, T // 2) for j in range(2)]
+        for j, tokens in enumerate(halves):
+            gated(gb_pair[:, 1, tokens], h[3], entries(pos2_t, j, j + 1, T // 2), g1[:, 1, tokens])
         for tokens in halves:
             nc.vector.tensor_tensor(
                 c_pair[:, tokens], ga_pair[:, :, tokens].rearrange("p t n -> p n t"), gb_pair[:, :, tokens].rearrange("p t n -> p n t"), ADD

@@ -24,7 +24,8 @@ ADD = mybir.AluOpType.add
 EARLY = 4
 BYTE_PIECES = ((0, 3), (3, 6), (6, 8))
 C_GROUPS = ((0, 2), (2, 4), (4, 6), (6, 7), (7, 8))
-PAIR_PIECES = ((0, 3), (3, 6), (6, 8))
+PAIR_PIECES = ((0, 2), (2, 4), (4, 6), (6, 8))
+OWN = 128
 OUT_PIECES = ((0, 3), (3, 4))
 
 
@@ -205,9 +206,8 @@ def tile_moe_ser_relu2_kernel(
 
         c_plane = [keep.tile([P, T], BF16, name=f"c{t}") for t in range(2)]
         c_pair = keep.tile([P, T, 2], BF16)
-        slot_pairs = keep.tile([P, 2, S], I32)
-        low_pairs = slot_pairs[:, 0, :].bitcast(BF16).rearrange("p (n t) -> p n t", t=2)
-        cq = keep.tile([P, S, 2], I32, align_bytes=64)
+        slot_pairs = {a: keep.tile([P, 2, (b - a) * C], I32, name=f"slot_pairs{a}") for a, b in PAIR_PIECES}
+        cq = {a: keep.tile([P, (b - a) * C, 2], I32, name=f"cq{a}", align_bytes=64) for a, b in PAIR_PIECES}
 
         def gated(dst, window, offsets, gate):
             nc.vector.tensor_tensor(dst, window[:].indirect(offsets), gate, MULT)
@@ -237,12 +237,13 @@ def tile_moe_ser_relu2_kernel(
             return back
 
         def gather_plane(t, first, last):
-            nc.scalar.activation(low_pairs[:, cols(first, last, C), t], c_plane[t][:].indirect(entries(offs2_t, first, last, C)), ACT.Copy)
+            low_pairs = slot_pairs[first][:, 0, :].bitcast(BF16).rearrange("p (n t) -> p n t", t=2)
+            nc.scalar.activation(low_pairs[:, :, t], c_plane[t][:].indirect(entries(offs2_t, first, last, C)), ACT.Copy)
 
         ident_bf = keep.tile([P, P], BF16)
         nc.scalar.copy(ident_bf[:], ident[:])
-        second_last = keep.tile([P, T], F32)
-        nc.scalar.activation(second_last[:], h[2][:].indirect(pos2_t[:]), ACT.Copy)
+        second_last = keep.tile([P, T - OWN], F32)
+        nc.scalar.activation(second_last[:], h[2][:].indirect(pos2_t[:, OWN // 16 :]), ACT.Copy)
         turned = round_sums(add_turned(0))
         turn(3, 4, 8, 2)
         back = turn_back(0, turned)
@@ -252,13 +253,15 @@ def tile_moe_ser_relu2_kernel(
         back = turn_back(1, round_sums(sums))
         gather_plane(0, *PAIR_PIECES[1])
         nc.scalar.copy(c_plane[1][:], back[:])
-        gather_plane(0, *PAIR_PIECES[2])
+        for piece in PAIR_PIECES[2:]:
+            gather_plane(0, *piece)
         for piece in PAIR_PIECES:
             gather_plane(1, *piece)
         ga_pair = keep.tile([P, 2, T], F32)
         gb_pair = keep.tile([P, 2, T], F32)
         gated(ga_pair[:, 0, :], h[2], pos1_t[:], g1[:, 0, :])
-        nc.vector.tensor_tensor(gb_pair[:, 0, :], second_last[:], g1[:, 1, :], MULT)
+        gated(gb_pair[:, 0, :OWN], h[2], pos2_t[:, : OWN // 16], g1[:, 1, :OWN])
+        nc.vector.tensor_tensor(gb_pair[:, 0, OWN:], second_last[:], g1[:, 1, OWN:], MULT)
         gated(ga_pair[:, 1, :], h[3], pos1_t[:], g1[:, 0, :])
         halves = [cols(j, j + 1, T // 2) for j in range(2)]
         for j, tokens in enumerate(halves):
@@ -275,14 +278,14 @@ def tile_moe_ser_relu2_kernel(
 
         def gather_pairs(first, last):
             nc.vector.tensor_copy(
-                slot_pairs[:, 1, cols(first, last, C)].bitcast(U32), pair_words.indirect(offs2_t[:, cols(first, last, C // 16)])
+                slot_pairs[first][:, 1, :].bitcast(U32), pair_words.indirect(offs2_t[:, cols(first, last, C // 16)])
             )
 
         def second_layer(first, last):
             slots = cols(first, last, C)
-            nc.vector.quantize_mx(
-                out=codes[:, slots].bitcast(FP8X4), scales=scales[:, slots], in_=cq[:, slots].rearrange("p n j -> p (n j)").bitcast(BF16)
-            )
+            start = max(a for a, _ in PAIR_PIECES if a <= first)
+            grouped = cq[start][:, cols(first - start, last - start, C)].rearrange("p n j -> p (n j)").bitcast(BF16)
+            nc.vector.quantize_mx(out=codes[:, slots].bitcast(FP8X4), scales=scales[:, slots], in_=grouped)
             bank = bank_tile((0, 1, 2, 7, 4)[C_GROUPS.index((first, last))])
             for f in range(first, last):
                 nc.tensor.matmul_mx(
@@ -298,13 +301,12 @@ def tile_moe_ser_relu2_kernel(
 
         for first, last in PAIR_PIECES:
             gather_pairs(first, last)
-        for first in range(0, E, 2):
-            slots = cols(first, first + 2, C)
-            pairs = slot_pairs[:, :, slots].rearrange("p j n -> p n j")
+        for first, last in PAIR_PIECES:
+            pairs = slot_pairs[first][:].rearrange("p j n -> p n j")
             if first >= E // 2:
-                nc.scalar.copy(cq[:, slots].bitcast(U32), pairs.bitcast(U32))
+                nc.scalar.copy(cq[first][:].bitcast(U32), pairs.bitcast(U32))
             else:
-                nc.vector.tensor_copy(cq[:, slots], pairs)
+                nc.vector.tensor_copy(cq[first][:], pairs)
         for group in C_GROUPS:
             second_layer(*group)
 

from contextlib import ExitStack

import concourse.mybir as mybir

K, T, E, C, H, N = 1536, 512, 8, 128, 512, 128
S = E * C
P = 128
PACK = 4
PASSES = K // (P * PACK)
FLOPS = 2 * S * (K * H + H * N)

F32 = mybir.dt.float32
BF16 = mybir.dt.bfloat16
I32 = mybir.dt.int32
U32 = mybir.dt.uint32
U16 = mybir.dt.uint16
U8 = mybir.dt.uint8
FP8X4 = mybir.dt.float8_e4m3fn_x4
FP4X4 = mybir.dt.float4_e2m1fn_x4
ACT = mybir.ActivationFunctionType
MULT = mybir.AluOpType.mult
ADD = mybir.AluOpType.add

EARLY = 4
BYTE_PIECES = ((0, 3), (3, 6), (6, 8))
C_GROUPS = ((0, 2), (2, 4), (4, 6), (6, 7), (7, 8))
PAIR_PIECES = ((0, 2), (2, 4), (4, 6), (6, 8))
OWN = 128
OUT_PIECES = ((0, 3), (3, 4))


def cols(first, last, width):
    return slice(first * width, last * width)


def tile_moe_ser_relu2_kernel(
    tc, x_words, x_scales, w1_words, w1_scales, w2_words, w2_scales, gate1, gate2, offs, pos1, pos2, offs2, pos3, pos4, out
):
    nc = tc.nc
    with ExitStack() as ctx:
        keep = ctx.enter_context(tc.tile_pool(name="keep", bufs=1))
        psum = ctx.enter_context(tc.psum_pool(name="psum", bufs=1))

        def load_list(name, dram):
            tile = keep.tile(list(dram.shape), U16, name=name)
            nc.sync.dma_start(tile[:], dram)
            return tile

        def load_scales(plane, dram):
            rows = dram.rearrange("g (q r) n -> r q g n", r=4)
            for r in range(4):
                nc.sync.dma_start(plane[r:P:32].bitcast(I32), rows[r].bitcast(I32))

        xs_a = keep.tile([P, T], U8, tag="shared_a", align_bytes=64)
        xs_b = keep.tile([P, T], U8, tag="shared_b", align_bytes=64)
        xs_moved = keep.tile([P, S], U8, align_bytes=64)
        head = EARLY * PASSES
        w1s_head = keep.tile([P, head, H], U8, align_bytes=64)
        w1s_rest = keep.tile([P, E * PASSES - head, H], U8, align_bytes=64)
        w2s = keep.tile([P, E, N], U8, align_bytes=64)
        nc.gpsimd.memset(xs_a[:].bitcast(I32), 0)
        nc.vector.memset(w1s_head[:].bitcast(I32), 0)
        nc.vector.memset(xs_b[:].bitcast(I32), 0)
        ones_raw = keep.tile([P, P], F32)
        nc.vector.memset(ones_raw[:], 1.0)
        nc.vector.memset(xs_moved[:].bitcast(I32), 0)
        nc.gpsimd.memset(w1s_rest[:].bitcast(I32), 0)

        offs_t = load_list("offs_t", offs)
        xw = [keep.tile([P, T], I32, name=f"xw{s}") for s in range(PASSES)]
        for s in range(PASSES):
            nc.sync.dma_start(xw[s][:], x_words[s].rearrange("p t d -> p (t d)").bitcast(I32))
        for q in range(4):
            nc.scalar.dma_start(xs_a[32 * q : 32 * q + 8].bitcast(I32), x_scales[0:PASSES:2, 4 * q : 4 * q + 4, :].bitcast(I32))
        w1_scale_rows = w1_scales.rearrange("e s b i -> (e s) b i")
        w1_rows = w1_words.rearrange("e s p n -> p (e s) n")
        w1 = [None] * (E * PASSES)

        def load_w1(first, last):
            tile = keep.tile([P, last - first, 2 * H], U8, name=f"w1_{first}", align_bytes=64)
            nc.sync.dma_start(tile[:].bitcast(I32), w1_rows[:, first:last, :].bitcast(I32))
            w1[first:last] = [tile[:, j, :] for j in range(last - first)]

        ones = keep.tile([P, P], F32)
        nc.scalar.activation(ones[:], ones_raw[:], ACT.Relu)
        nc.vector.memset(w2s[:].bitcast(I32), 0)
        load_scales(w1s_head, w1_scale_rows[:head])
        pass1_rows = x_scales[1].rearrange("(q r) n -> r q n", r=4)
        for r in range(4):
            nc.sync.dma_start(xs_b[r:P:32].bitcast(I32), pass1_rows[r].bitcast(I32))
        for e in range(EARLY):
            load_w1(e * PASSES, (e + 1) * PASSES)

        def entries(tile, first, last, width):
            return tile[:, cols(first, last, width // 16)]

        xs_g = keep.tile([P, S], U8, align_bytes=64)
        xs_gb = keep.tile([P, S], U8, align_bytes=64)
        relu = [keep.tile([P, PACK, P], F32, name=f"relu{e}") for e in range(E)]
        h = [keep.tile([P, S], F32, name=f"h{t}") for t in range(PACK)]

        def bank_tile(b):
            return psum.tile([P, H], F32, name=f"bank{b}")

        def gather_words(dst, s, first, last):
            nc.vector.tensor_copy(dst, xw[s][:].bitcast(U32).indirect(offs_t[:, cols(first, last, C // 16)]))

        def turn(t, first, last, b):
            bank = bank_tile(b)
            for e in range(first, last):
                nc.tensor.transpose(bank[:, cols(e - first, e - first + 1, C)], relu[e][:, t, :], ident[:])
            nc.scalar.activation(h[t][:, cols(first, last, C)], bank[:, cols(0, last - first, C)], ACT.Square)

        xw_first = keep.tile([P, 2 * C], U32, align_bytes=64)
        gather_words(xw_first[:], 0, 0, 2)
        for first, last in BYTE_PIECES:
            nc.vector.tensor_copy(xs_g[:, cols(first, last, C)], xs_a[:].indirect(offs_t[:, cols(first, last, C // 16)]))
        rest_rows = w1_scale_rows[head:].rearrange("g (q r) n -> r q g n", r=4)
        for m in range(4):
            nc.sync.dma_start(xs_moved[m:P:32].bitcast(I32), xs_g[4 + m : P : 32].bitcast(I32))
        for r in range(4):
            nc.sync.dma_start(w1s_rest[r:P:32].bitcast(I32), rest_rows[r].bitcast(I32))
        for e in range(EARLY, 6):
            load_w1(e * PASSES, (e + 1) * PASSES)
        load_w1(18, 22)
        load_w1(22, 23)
        load_w1(23, 24)
        pos1_t = load_list("pos1_t", pos1)
        pos2_t = load_list("pos2_t", pos2)
        g1 = keep.tile([P, 2, T], F32)
        for r in range(2):
            nc.sync.dma_start(g1[:, r, :], gate1[r])
        offs2_t = load_list("offs2_t", offs2)
        w2 = keep.tile([P, E, N], I32, align_bytes=64)
        nc.sync.dma_start(w2[:], w2_words.rearrange("f s p n d -> p (f s) (n d)").bitcast(I32))
        load_scales(w2s, w2_scales.rearrange("f s b n -> (f s) b n"))
        pos3_t = load_list("pos3_t", pos3)
        pos4_t = load_list("pos4_t", pos4)
        g2 = keep.tile([P, 2, T], F32)
        nc.sync.dma_start(g2[:], gate2.rearrange("r p t -> p r t"))

        xw_next = keep.tile([P, (PASSES - 1) * 2 * C], U32, tag="shared_a", align_bytes=64)
        for s in range(1, PASSES):
            gather_words(xw_next[:, cols(2 * s - 2, 2 * s, C)], s, 0, 2)
        for first, last in BYTE_PIECES:
            nc.vector.tensor_copy(xs_gb[:, cols(first, last, C)], xs_b[:].indirect(offs_t[:, cols(first, last, C // 16)]))
        xw_late = keep.tile([P, PASSES * (E - 2) * C], U32, tag="shared_b", align_bytes=64)

        def words(s, first, last):
            if first >= 2:
                return xw_late[:, cols(s * (E - 2) - 2 + first, s * (E - 2) - 2 + last, C)]
            if s == 0:
                return xw_first[:, cols(first, last, C)]
            return xw_next[:, cols(2 * s - 2 + first, 2 * s - 2 + last, C)]

        for first, last in ((2, 4), (4, 6), (6, 7), (7, 8)):
            for s in range(PASSES):
                gather_words(words(s, first, last), s, first, last)

        def one_pass(acc, e, s):
            nc.tensor.matmul_mx(
                out=acc[:],
                lhsT=words(s, e, e + 1).bitcast(FP8X4),
                lhsT_scale=(xs_g, xs_gb, xs_moved)[s][:, cols(e, e + 1, C)],
                rhs=w1[e * PASSES + s].bitcast(FP4X4),
                rhs_scale=w1s_head[:, e * PASSES + s, :] if e < EARLY else w1s_rest[:, e * PASSES + s - head, :],
                start=(s == 0),
                stop=(s == PASSES - 1),
            )

        def rectify(e, acc, planes):
            by_plane = acc[:].rearrange("p (m t) -> p t m", t=PACK)[:, planes, :]
            if e == 7:
                nc.vector.tensor_scalar_max(relu[e][:, planes, :], by_plane, 0.0)
            else:
                nc.scalar.activation(relu[e][:, planes, :], by_plane, ACT.Relu)

        banks = [bank_tile(b) for b in (0, 1, 2, 3, 5, 6, 7)]
        for first in range(0, EARLY, 2):
            for s in range(PASSES - 1):
                for e in range(first, first + 2):
                    one_pass(banks[e], e, s)
        for e in range(EARLY):
            one_pass(banks[e], e, PASSES - 1)
            rectify(e, banks[e], slice(0, PACK))
        for e in range(EARLY, 6):
            for s in range(PASSES):
                one_pass(banks[e], e, s)
            rectify(e, banks[e], slice(0, PACK))
        ident = keep.tile([P, P], F32, name=f"w1_{head}", align_bytes=64)
        nc.gpsimd.affine_select(
            out=ident[:], in_=ones[:], compare_op=mybir.AluOpType.is_equal, fill=0.0, base=0, pattern=[[-1, P]], channel_multiplier=1
        )
        turn(0, 0, EARLY, 4)
        for e in range(6, E):
            acc = banks[e] if e == 6 else bank_tile(0)
            for s in range(PASSES):
                one_pass(acc, e, s)
            rectify(e, acc, slice(0, 1))
            if e == E - 1:
                turn(0, 4, 7, 1)
                turn(0, 7, 8, 2)
            rectify(e, acc, slice(1, PACK))
        for j in range(2, 2 * PACK - 1):
            turn(j // 2, 4 * (j % 2), 4 * (j % 2) + 4, (j - 1) % 3)

        c_plane = [keep.tile([P, T], BF16, name=f"c{t}") for t in range(2)]
        c_pair = keep.tile([P, T, 2], BF16)
        slot_pairs = {a: keep.tile([P, 2, (b - a) * C], I32, name=f"slot_pairs{a}") for a, b in PAIR_PIECES}
        cq = {a: keep.tile([P, (b - a) * C, 2], I32, name=f"cq{a}", align_bytes=64) for a, b in PAIR_PIECES}

        def gated(dst, window, offsets, gate):
            nc.vector.tensor_tensor(dst, window[:].indirect(offsets), gate, MULT)

        def add_turned(t):
            ga = keep.tile([P, T], F32, name=f"ga{t}")
            gb = keep.tile([P, T], F32, name=f"gb{t}")
            gated(ga[:], h[t], pos1_t[:], g1[:, 0, :])
            gated(gb[:], h[t], pos2_t[:], g1[:, 1, :])
            sums = bank_tile(1)
            for b in range(T // P):
                block = cols(b, b + 1, P)
                nc.tensor.matmul(sums[:, block], ga[:, block], ident[:], start=True, stop=False, is_transpose=True)
                nc.tensor.matmul(sums[:, block], gb[:, block], ident[:], start=False, stop=True, is_transpose=True)
            return sums

        def round_sums(sums):
            turned = keep.tile([P, T], BF16, name="turned")
            nc.scalar.copy(turned[:], sums[:])
            return turned

        def turn_back(t, turned):
            back = psum.tile([P, T], BF16, name=f"bank{5 + t}")
            for b in range(T // P):
                block = cols(b, b + 1, P)
                nc.tensor.transpose(back[:, block], turned[:, block], ident_bf[:])
            return back

        def gather_plane(t, first, last):
            low_pairs = slot_pairs[first][:, 0, :].bitcast(BF16).rearrange("p (n t) -> p n t", t=2)
            nc.scalar.activation(low_pairs[:, :, t], c_plane[t][:].indirect(entries(offs2_t, first, last, C)), ACT.Copy)

        ident_bf = keep.tile([P, P], BF16)
        nc.scalar.copy(ident_bf[:], ident[:])
        second_last = keep.tile([P, T - OWN], F32)
        nc.scalar.activation(second_last[:], h[2][:].indirect(pos2_t[:, OWN // 16 :]), ACT.Copy)
        turned = round_sums(add_turned(0))
        turn(3, 4, 8, 2)
        back = turn_back(0, turned)
        sums = add_turned(1)
        nc.scalar.copy(c_plane[0][:], back[:])
        gather_plane(0, *PAIR_PIECES[0])
        back = turn_back(1, round_sums(sums))
        gather_plane(0, *PAIR_PIECES[1])
        nc.scalar.copy(c_plane[1][:], back[:])
        for piece in PAIR_PIECES[2:]:
            gather_plane(0, *piece)
        for piece in PAIR_PIECES:
            gather_plane(1, *piece)
        ga_pair = keep.tile([P, 2, T], F32)
        gb_pair = keep.tile([P, 2, T], F32)
        gated(ga_pair[:, 0, :], h[2], pos1_t[:], g1[:, 0, :])
        gated(gb_pair[:, 0, :OWN], h[2], pos2_t[:, : OWN // 16], g1[:, 1, :OWN])
        nc.vector.tensor_tensor(gb_pair[:, 0, OWN:], second_last[:], g1[:, 1, OWN:], MULT)
        gated(ga_pair[:, 1, :], h[3], pos1_t[:], g1[:, 0, :])
        halves = [cols(j, j + 1, T // 2) for j in range(2)]
        for j, tokens in enumerate(halves):
            gated(gb_pair[:, 1, tokens], h[3], entries(pos2_t, j, j + 1, T // 2), g1[:, 1, tokens])
        for tokens in halves:
            nc.vector.tensor_tensor(
                c_pair[:, tokens], ga_pair[:, :, tokens].rearrange("p t n -> p n t"), gb_pair[:, :, tokens].rearrange("p t n -> p n t"), ADD
            )

        codes = keep.tile([P, S], U32, align_bytes=64)
        scales = keep.tile([P, S], U8, align_bytes=64)
        y = keep.tile([P, S], F32)
        pair_words = c_pair[:].rearrange("p n t -> p (n t)").bitcast(U32)

        def gather_pairs(first, last):
            nc.vector.tensor_copy(
                slot_pairs[first][:, 1, :].bitcast(U32), pair_words.indirect(offs2_t[:, cols(first, last, C // 16)])
            )

        def second_layer(first, last):
            slots = cols(first, last, C)
            start = max(a for a, _ in PAIR_PIECES if a <= first)
            grouped = cq[start][:, cols(first - start, last - start, C)].rearrange("p n j -> p (n j)").bitcast(BF16)
            nc.vector.quantize_mx(out=codes[:, slots].bitcast(FP8X4), scales=scales[:, slots], in_=grouped)
            bank = bank_tile((0, 1, 2, 7, 4)[C_GROUPS.index((first, last))])
            for f in range(first, last):
                nc.tensor.matmul_mx(
                    out=bank[:, cols(f - first, f - first + 1, C)],
                    lhsT=w2[:, f, :].bitcast(FP8X4),
                    lhsT_scale=w2s[:, f, :],
                    rhs=codes[:, cols(f, f + 1, C)].bitcast(FP8X4),
                    rhs_scale=scales[:, cols(f, f + 1, C)],
                    start=True,
                    stop=True,
                )
            nc.scalar.copy(y[:, slots], bank[:, cols(0, last - first, C)])

        for first, last in PAIR_PIECES:
            gather_pairs(first, last)
        for first, last in PAIR_PIECES:
            pairs = slot_pairs[first][:].rearrange("p j n -> p n j")
            if first >= E // 2:
                nc.scalar.copy(cq[first][:].bitcast(U32), pairs.bitcast(U32))
            else:
                nc.vector.tensor_copy(cq[first][:], pairs)
        for group in C_GROUPS:
            second_layer(*group)

        ya = keep.tile([P, T], F32)
        yb = keep.tile([P, T], F32)
        res = keep.tile([P, T], F32)

        def finish(first, last):
            tokens = cols(first, last, P)
            nc.vector.tensor_tensor(res[:, tokens], ya[:, tokens], yb[:, tokens], ADD)
            nc.sync.dma_start(out[:, tokens], res[:, tokens])

        fetched = keep.tile([P, T], F32)
        for first, last in OUT_PIECES:
            tokens = cols(first, last, P)
            nc.scalar.activation(fetched[:, tokens], y[:].indirect(pos4_t[:, cols(first, last, P // 16)]), ACT.Copy)
            gated(ya[:, tokens], y, pos3_t[:, cols(first, last, P // 16)], g2[:, 0, tokens])
        for first, last in OUT_PIECES:
            tokens = cols(first, last, P)
            nc.vector.tensor_tensor(yb[:, tokens], fetched[:, tokens], g2[:, 1, tokens], MULT)
        for piece in OUT_PIECES:
            finish(*piece)
